import numpy as np
import ml_dtypes


def mxq(x, axis, fmt="e4m3"):
    dtype, down = {"e4m3": (ml_dtypes.float8_e4m3fn, 7), "e5m2": (ml_dtypes.float8_e5m2, 14)}[fmt]
    v = np.moveaxis(np.asarray(x, np.float32).astype(ml_dtypes.bfloat16).astype(np.float64), axis, -1)
    blocks = v.reshape(v.shape[:-1] + (-1, 32))
    amax = np.abs(blocks).max(-1, keepdims=True)
    byte = np.maximum(np.where(amax > 0, np.frexp(amax)[1] - 1 + 127, 0) - down, 1)
    scale = np.exp2(byte - 127.0)
    codes = (blocks / scale).astype(np.float32).astype(dtype).astype(np.float64)
    return np.moveaxis((codes * scale).reshape(v.shape), -1, axis)


WIDE = False


def mx_kscale(k):
    if not WIDE:
        return np.ones(k)
    levels = np.array([10, -10, 5, -5, 0])
    if k % 512:
        return np.exp2(np.random.permutation(np.resize(levels, k // 32))).repeat(32)
    a = np.empty((k // 512, 16))
    for p in range(k // 512):
        a[p, :8] = np.random.permutation(np.resize(levels, 8))
        for g in range(8):
            far = levels[np.abs(levels - a[p, g]) >= 10]
            a[p, g + 8] = far[np.random.randint(len(far))]
    return np.exp2(a.ravel()).repeat(32)


def f64(x):
    return np.asarray(x).astype(np.float64)


def striped(idx):
    return np.tile(idx.reshape(-1, 16).T, (8, 1)).astype(np.uint16)


def unstriped(offs):
    return offs[:16].T.reshape(-1).astype(np.int64)


E2M1 = np.array([0.0, 0.5, 1.0, 1.5, 2.0, 3.0, 4.0, 6.0, -0.0, -0.5, -1.0, -1.5, -2.0, -3.0, -4.0, -6.0])


def pack_weight(w, fmt):
    k, n = w.shape
    w = f64(np.asarray(w, np.float32).astype(ml_dtypes.bfloat16)).reshape(k // 32, 32, n)
    amax = np.abs(w).max(1)
    if fmt == "e4m3":
        byte = np.frexp(amax)[1] - 1 + 127 - 7
    else:
        mant, ex = np.frexp(amax / 6.0)
        byte = np.where(mant > 0.5, ex, ex - 1) + 127
    byte = np.clip(np.where(amax > 0, byte, 1), 1, 254)
    scaled = (w * np.exp2(127.0 - byte)[:, None, :]).reshape(k, n).astype(np.float32)
    by_word = np.ascontiguousarray(scaled.reshape(k // 512, 128, 4, n).transpose(0, 1, 3, 2))
    if fmt == "e4m3":
        words = by_word.astype(ml_dtypes.float8_e4m3fn).view(np.uint8)
    else:
        c = by_word.astype(ml_dtypes.float4_e2m1fn).view(np.uint8) & 0xF
        words = (c[..., 0::2] | (c[..., 1::2] << 4)).reshape(k // 512, 128, 2 * n)
    return np.ascontiguousarray(words), np.ascontiguousarray(byte.astype(np.uint8).reshape(k // 512, 16, n))


def unpack_weight(words, scales, fmt):
    g, _, n = scales.shape
    words = np.ascontiguousarray(words).reshape(g, 128, n, -1)
    if fmt == "e4m3":
        vals = words.view(ml_dtypes.float8_e4m3fn).astype(np.float64)
    else:
        nib = np.empty((g, 128, n, 4), np.uint8)
        nib[..., 0::2] = words & 0xF
        nib[..., 1::2] = words >> 4
        vals = E2M1[nib]
    vals = vals * np.repeat(np.exp2(scales.astype(np.float64) - 127.0), 8, axis=1)[..., None]
    return vals.transpose(0, 1, 3, 2).reshape(g * 512, n)


def relu(v):
    return np.maximum(v, 0.0)


K, T, E, C, N = 1024, 1024, 4, 256, 512


def by_slot(wq, xq):
    return np.concatenate([xq[:, e * C:(e + 1) * C].T @ wq[e] for e in range(E)])


def setup_inputs():
    n = np.random.standard_normal
    s = mx_kscale(K)
    slot_token = np.concatenate([np.random.permutation(T)[:C] for e in range(E)])
    x = pack_weight(n((K, T)) * s[:, None], "e2m1")
    two = np.ascontiguousarray(x[0].reshape(K // 1024, 2, 128, T, 2).transpose(0, 2, 3, 1, 4).reshape(K // 1024, 128, T, 4))
    return {
        "x_words": two,
        "x_scales": x[1],
        "w": (n((E, K, N)) / np.sqrt(K) / s[None, :, None]).astype(np.float32),
        "offs": striped(slot_token),
    }


def reference(x_words, x_scales, w, offs):
    wq = mxq(f64(w), 1, "e4m3")
    idx = unstriped(offs)
    words = x_words.reshape(K // 1024, 128, T, 2, 2).transpose(0, 3, 1, 2, 4).reshape(K // 512, 128, 2 * T)
    xq = unpack_weight(words, x_scales, "e2m1")[:, idx]
    y = relu(by_slot(wq, xq))
    return y

@@ -1,0 +1,154 @@
+from contextlib import ExitStack
+
+import concourse.mybir as mybir
+
+K, T, E, C, N = 1024, 1024, 4, 256, 512
+FLOPS = 2 * E * C * K * N
+
+F32 = mybir.dt.float32
+BF16 = mybir.dt.bfloat16
+I32 = mybir.dt.int32
+U32 = mybir.dt.uint32
+U16 = mybir.dt.uint16
+U8 = mybir.dt.uint8
+FP8X4 = mybir.dt.float8_e4m3fn_x4
+FP4X4 = mybir.dt.float4_e2m1fn_x4
+RELU = mybir.ActivationFunctionType.Relu
+
+P = 128
+PACK = 4
+K_PASS = P * PACK
+PASSES = K // K_PASS
+GROUP = 16
+SLOT_TILES = C // P
+OVERLAP = 8
+PIECES = [(0, 0, 0, 256), (0, 0, 256, 512), (0, 1, 0, 512), (1, 0, 0, 512), (1, 1, 0, 512), (2, 0, 0, 512), (2, 1, 0, 512), (3, 0, 0, 512), (3, 1, 0, 256), (3, 1, 256, 512)]
+VECTOR_COLUMNS = [160, 160, 192, 192, 192, 192, 256, 256, 176, 176]
+TOKEN_STEPS = [
+    ([], []),
+    ([], [("scales", 0, 512), ("scales", 512, 1024), ("words", 0, 512)]),
+    ([("part", 0, 512)], []),
+    ([("words", 512, 768)], []),
+    ([("words", 768, 1024)], []),
+    ([("part", 512, 1024)], []),
+    ([], []),
+    ([], []),
+    ([], []),
+    ([], []),
+]
+STORES = {3: 0, 5: 4, 6: 6, 7: 7}
+
+
+def interleave(copy, grouped, raw, c0, c1):
+    copy(
+        out=grouped[:, c0:c1, :].rearrange("p (c i) t -> p c t i", i=4),
+        in_=raw[:, :, c0:c1].rearrange("p t (c i) -> p c t i", i=4),
+    )
+
+
+def tile_moe_s_lin_relu_kernel(tc, x_words, x_scales, w, offs, out):
+    nc = tc.nc
+    with ExitStack() as ctx:
+        keep = ctx.enter_context(tc.tile_pool(name="keep", bufs=1))
+        psum = ctx.enter_context(tc.psum_pool(name="psum", bufs=1))
+
+        raws = []
+
+        def load(i):
+            e, g, n0, n1 = PIECES[i]
+            raw = keep.tile([P, PACK, n1 - n0], F32, name="raw_%d" % i)
+            nc.sync.dma_start(raw[:], w[e, g * K_PASS : (g + 1) * K_PASS, n0:n1].rearrange("(p j) n -> p j n", j=PACK))
+            raws.append(raw)
+
+        for i in range(2):
+            load(i)
+        offsets = keep.tile([P, E * C // GROUP], U16, name="offsets")
+        nc.sync.dma_start(offsets[:], offs)
+        token_scales = keep.tile([P, T], U8, name="token_scales", align_bytes=64)
+        nc.vector.memset(token_scales[:].bitcast(I32), 0)
+        for q in range(4):
+            nc.sync.dma_start(
+                token_scales[32 * q : 32 * q + 4 * PASSES, :].bitcast(I32),
+                x_scales[:, 4 * q : 4 * q + 4, :].bitcast(I32),
+            )
+        token_words = keep.tile([P, T], I32, name="token_words", align_bytes=64)
+        nc.sync.dma_start(token_words[:], x_words[0].rearrange("p t d -> p (t d)").bitcast(I32))
+        for i in range(2, len(PIECES)):
+            load(i)
+
+        pair_words = keep.tile([P, E * C], I32, name="pair_words", align_bytes=64)
+        slot_words = keep.tile([P, PASSES, 2 * E * C], U8, name="slot_words", align_bytes=64)
+        slot_scales = [keep.tile([P, E * C], U8, name="slot_scales_%d" % g, align_bytes=64) for g in range(PASSES)]
+        nc.vector.memset(slot_scales[1][:].bitcast(I32), 0)
+
+        def token_step(kind, s0, s1):
+            mine = offsets[:, s0 // GROUP : s1 // GROUP]
+            if kind == "words":
+                nc.vector.tensor_copy(pair_words[:, s0:s1].bitcast(U32), token_words[:].bitcast(U32).indirect(mine))
+            elif kind == "part":
+                nc.vector.tensor_copy(
+                    slot_words[:].bitcast(U16)[:, :, s0:s1],
+                    pair_words[:, s0:s1].bitcast(U16).rearrange("p (c g) -> p g c", g=PASSES),
+                )
+            else:
+                nc.vector.tensor_copy(slot_scales[0][:, s0:s1], token_scales[:].indirect(mine))
+                if s1 == E * C:
+                    nc.gpsimd.dma_start(slot_scales[1][0 : 100, :].bitcast(I32), slot_scales[0][4 : 100 + 4, :].bitcast(I32))
+
+        staged = keep.tile([P, 2 * N - OVERLAP, PACK], BF16, name="staged", align_bytes=64)
+        codes = keep.tile([P, E * PASSES, N], U32, name="codes", align_bytes=64)
+        scales = keep.tile([P, E * PASSES, N], U8, name="scales", align_bytes=64)
+        results = keep.tile([P, E * SLOT_TILES, N], F32, name="results")
+        banks = [psum.tile([P, N], F32, name="bank_%d" % b) for b in range(E * SLOT_TILES)]
+        out_tiles = out.rearrange("(s p) n -> p s n", p=P)
+
+        def multiply(e, g):
+            for tile in range(e * SLOT_TILES, (e + 1) * SLOT_TILES):
+                nc.tensor.matmul_mx(
+                    out=banks[tile][:],
+                    lhsT=slot_words[:, g, 2 * tile * P : 2 * (tile + 1) * P].bitcast(FP4X4),
+                    lhsT_scale=slot_scales[g][:, tile * P : (tile + 1) * P],
+                    rhs=codes[:, e * PASSES + g, :].bitcast(FP8X4),
+                    rhs_scale=scales[:, e * PASSES + g, :],
+                    start=(g == 0),
+                    stop=(g == PASSES - 1),
+                )
+
+        def finish(e):
+            for tile in range(e * SLOT_TILES, (e + 1) * SLOT_TILES):
+                if tile == E * SLOT_TILES - 1:
+                    nc.vector.tensor_scalar_max(results[:, tile, :], banks[tile][:], 0.0)
+                else:
+                    nc.scalar.activation(results[:, tile, :], banks[tile][:], RELU)
+                if tile in STORES:
+                    first = STORES[tile]
+                    nc.sync.dma_start(out_tiles[:, first : tile + 1, :], results[:, first : tile + 1, :])
+
+        for i, (e, g, n0, n1) in enumerate(PIECES):
+            width = n1 - n0
+            share = VECTOR_COLUMNS[i]
+            if i % 2 == 0:
+                grouped = staged[:, N - width : N, :]
+                on_scalar, on_vector = (0, width - share), (width - share, width)
+            else:
+                grouped = staged[:, N - OVERLAP : N - OVERLAP + width, :]
+                on_scalar, on_vector = (share, width), (0, share)
+            if share < width:
+                interleave(nc.scalar.copy, grouped, raws[i], *on_scalar)
+            interleave(nc.vector.tensor_copy, grouped, raws[i], *on_vector)
+            before, after = TOKEN_STEPS[i]
+            for step in before:
+                token_step(*step)
+            nc.vector.quantize_mx(
+                out=codes[:, e * PASSES + g, n0:n1].bitcast(FP8X4),
+                scales=scales[:, e * PASSES + g, n0:n1],
+                in_=grouped.rearrange("p n t -> p (n t)"),
+            )
+            for step in after:
+                token_step(*step)
+            if i == 2:
+                multiply(0, 0)
+            if n1 == N and i > 1:
+                multiply(e, g)
+                if g == PASSES - 1:
+                    finish(e)

@@ -23,10 +23,10 @@ GROUP = 16
 SLOT_TILES = C // P
 OVERLAP = 8
 PIECES = [(0, 0, 0, 256), (0, 0, 256, 512), (0, 1, 0, 512), (1, 0, 0, 512), (1, 1, 0, 512), (2, 0, 0, 512), (2, 1, 0, 512), (3, 0, 0, 512), (3, 1, 0, 256), (3, 1, 256, 512)]
-VECTOR_COLUMNS = [160, 160, 192, 192, 192, 192, 256, 256, 176, 176]
+VECTOR_COLUMNS = [160, 32, 192, 192, 192, 192, 256, 256, 176, 176]
 TOKEN_STEPS = [
-    ([], []),
-    ([], [("scales", 0, 512), ("scales", 512, 1024), ("words", 0, 512)]),
+    ([], [("scales", 0, 512), ("scales", 512, 1024)]),
+    ([], [("words", 0, 512)]),
     ([("part", 0, 512)], []),
     ([("words", 512, 768)], []),
     ([("words", 768, 1024)], []),
@@ -60,10 +60,9 @@ def tile_moe_s_lin_relu_kernel(tc, x_words, x_scales, w, offs, out):
             nc.sync.dma_start(raw[:], w[e, g * K_PASS : (g + 1) * K_PASS, n0:n1].rearrange("(p j) n -> p j n", j=PACK))
             raws.append(raw)
 
-        for i in range(2):
-            load(i)
         offsets = keep.tile([P, E * C // GROUP], U16, name="offsets")
         nc.sync.dma_start(offsets[:], offs)
+        load(0)
         token_scales = keep.tile([P, T], U8, name="token_scales", align_bytes=64)
         nc.vector.memset(token_scales[:].bitcast(I32), 0)
         for q in range(4):
@@ -71,6 +70,7 @@ def tile_moe_s_lin_relu_kernel(tc, x_words, x_scales, w, offs, out):
                 token_scales[32 * q : 32 * q + 4 * PASSES, :].bitcast(I32),
                 x_scales[:, 4 * q : 4 * q + 4, :].bitcast(I32),
             )
+        load(1)
         token_words = keep.tile([P, T], I32, name="token_words", align_bytes=64)
         nc.sync.dma_start(token_words[:], x_words[0].rearrange("p t d -> p (t d)").bitcast(I32))
         for i in range(2, len(PIECES)):
@@ -93,7 +93,7 @@ def tile_moe_s_lin_relu_kernel(tc, x_words, x_scales, w, offs, out):
             else:
                 nc.vector.tensor_copy(slot_scales[0][:, s0:s1], token_scales[:].indirect(mine))
                 if s1 == E * C:
-                    nc.gpsimd.dma_start(slot_scales[1][0 : 100, :].bitcast(I32), slot_scales[0][4 : 100 + 4, :].bitcast(I32))
+                    nc.scalar.dma_start(slot_scales[1][0 : 112, :].bitcast(I32), slot_scales[0][4 : 112 + 4, :].bitcast(I32))
 
         staged = keep.tile([P, 2 * N - OVERLAP, PACK], BF16, name="staged", align_bytes=64)
         codes = keep.tile([P, E * PASSES, N], U32, name="codes", align_bytes=64)

@@ -21,22 +21,11 @@ K_PASS = P * PACK
 PASSES = K // K_PASS
 GROUP = 16
 SLOT_TILES = C // P
-OVERLAP = 8
+STAGED_AT = [512, 768, 0, 512, 0, 512, 0, 504, 0, 760]
+EARLY = 4
 PIECES = [(0, 0, 0, 256), (0, 0, 256, 512), (0, 1, 0, 512), (1, 0, 0, 512), (1, 1, 0, 512), (2, 0, 0, 512), (2, 1, 0, 512), (3, 0, 0, 512), (3, 1, 0, 256), (3, 1, 256, 512)]
-VECTOR_COLUMNS = [160, 32, 192, 192, 192, 192, 256, 256, 176, 176]
-TOKEN_STEPS = [
-    ([], [("scales", 0, 512), ("scales", 512, 1024)]),
-    ([], [("words", 0, 512)]),
-    ([("part", 0, 512)], []),
-    ([("words", 512, 768)], []),
-    ([("words", 768, 1024)], []),
-    ([("part", 512, 1024)], []),
-    ([], []),
-    ([], []),
-    ([], []),
-    ([], []),
-]
-STORES = {3: 0, 5: 4, 6: 6, 7: 7}
+VECTOR_COLUMNS = [0, 0, 192, 192, 192, 192, 256, 320, 176, 176]
+RESULT_ON = [4, 6, 9]
 
 
 def interleave(copy, grouped, raw, c0, c1):
@@ -54,30 +43,35 @@ def tile_moe_s_lin_relu_kernel(tc, x_words, x_scales, w, offs, out):
 
         raws = []
 
-        def load(i):
+        def part(tile, first, i):
+            at = PACK * sum(n1 - n0 for e, g, n0, n1 in PIECES[first:i])
+            width = PIECES[i][3] - PIECES[i][2]
+            return tile[:, at : at + PACK * width].rearrange("p (j n) -> p j n", j=PACK)
+
+        def load(i, raw):
             e, g, n0, n1 = PIECES[i]
-            raw = keep.tile([P, PACK, n1 - n0], F32, name="raw_%d" % i)
-            nc.sync.dma_start(raw[:], w[e, g * K_PASS : (g + 1) * K_PASS, n0:n1].rearrange("(p j) n -> p j n", j=PACK))
+            nc.sync.dma_start(raw, w[e, g * K_PASS : (g + 1) * K_PASS, n0:n1].rearrange("(p j) n -> p j n", j=PACK))
             raws.append(raw)
 
         offsets = keep.tile([P, E * C // GROUP], U16, name="offsets")
         nc.sync.dma_start(offsets[:], offs)
-        load(0)
-        token_scales = keep.tile([P, T], U8, name="token_scales", align_bytes=64)
+        early = keep.tile([P, PACK * sum(n1 - n0 for e, g, n0, n1 in PIECES[:EARLY])], F32, name="early")
+        load(0, part(early, 0, 0))
+        token_scales = keep.tile([P, T], U8, name="token_scales", tag="reused", align_bytes=64)
         nc.vector.memset(token_scales[:].bitcast(I32), 0)
         for q in range(4):
             nc.sync.dma_start(
                 token_scales[32 * q : 32 * q + 4 * PASSES, :].bitcast(I32),
                 x_scales[:, 4 * q : 4 * q + 4, :].bitcast(I32),
             )
-        load(1)
+        load(1, part(early, 0, 1))
         token_words = keep.tile([P, T], I32, name="token_words", align_bytes=64)
         nc.sync.dma_start(token_words[:], x_words[0].rearrange("p t d -> p (t d)").bitcast(I32))
-        for i in range(2, len(PIECES)):
-            load(i)
+        for i in range(2, EARLY):
+            load(i, part(early, 0, i))
 
         pair_words = keep.tile([P, E * C], I32, name="pair_words", align_bytes=64)
-        slot_words = keep.tile([P, PASSES, 2 * E * C], U8, name="slot_words", align_bytes=64)
+        slot_words = [keep.tile([P, PASSES, E * C], U8, name="slot_words_%d" % h, align_bytes=64) for h in range(2)]
         slot_scales = [keep.tile([P, E * C], U8, name="slot_scales_%d" % g, align_bytes=64) for g in range(PASSES)]
         nc.vector.memset(slot_scales[1][:].bitcast(I32), 0)
 
@@ -87,18 +81,25 @@ def tile_moe_s_lin_relu_kernel(tc, x_words, x_scales, w, offs, out):
                 nc.vector.tensor_copy(pair_words[:, s0:s1].bitcast(U32), token_words[:].bitcast(U32).indirect(mine))
             elif kind == "part":
                 nc.vector.tensor_copy(
-                    slot_words[:].bitcast(U16)[:, :, s0:s1],
+                    slot_words[s0 // (2 * C)][:].bitcast(U16),
                     pair_words[:, s0:s1].bitcast(U16).rearrange("p (c g) -> p g c", g=PASSES),
                 )
             else:
                 nc.vector.tensor_copy(slot_scales[0][:, s0:s1], token_scales[:].indirect(mine))
                 if s1 == E * C:
-                    nc.scalar.dma_start(slot_scales[1][0 : 112, :].bitcast(I32), slot_scales[0][4 : 112 + 4, :].bitcast(I32))
+                    nc.sync.dma_start(slot_scales[1][0 : 112, :].bitcast(I32), slot_scales[0][4 : 112 + 4, :].bitcast(I32))
 
-        staged = keep.tile([P, 2 * N - OVERLAP, PACK], BF16, name="staged", align_bytes=64)
+        token_step("scales", 0, 512)
+        token_step("scales", 512, 1024)
+        late = keep.tile([P, PACK * sum(n1 - n0 for e, g, n0, n1 in PIECES[EARLY:])], F32, name="late", tag="reused", align_bytes=64)
+        for i in range(EARLY, len(PIECES)):
+            load(i, part(late, EARLY, i))
+
+        staged = keep.tile([P, 2 * N, PACK], BF16, name="staged", align_bytes=64)
         codes = keep.tile([P, E * PASSES, N], U32, name="codes", align_bytes=64)
         scales = keep.tile([P, E * PASSES, N], U8, name="scales", align_bytes=64)
-        results = keep.tile([P, E * SLOT_TILES, N], F32, name="results")
+        last = keep.tile([P, SLOT_TILES * N], F32, name="last")
+        results = [raws[i].rearrange("p j n -> p (j n)")[:, 0 : SLOT_TILES * N] for i in RESULT_ON] + [last[:]]
         banks = [psum.tile([P, N], F32, name="bank_%d" % b) for b in range(E * SLOT_TILES)]
         out_tiles = out.rearrange("(s p) n -> p s n", p=P)
 
@@ -106,7 +107,7 @@ def tile_moe_s_lin_relu_kernel(tc, x_words, x_scales, w, offs, out):
             for tile in range(e * SLOT_TILES, (e + 1) * SLOT_TILES):
                 nc.tensor.matmul_mx(
                     out=banks[tile][:],
-                    lhsT=slot_words[:, g, 2 * tile * P : 2 * (tile + 1) * P].bitcast(FP4X4),
+                    lhsT=slot_words[tile // 4][:, g, 2 * (tile % 4) * P : 2 * (tile % 4 + 1) * P].bitcast(FP4X4),
                     lhsT_scale=slot_scales[g][:, tile * P : (tile + 1) * P],
                     rhs=codes[:, e * PASSES + g, :].bitcast(FP8X4),
                     rhs_scale=scales[:, e * PASSES + g, :],
@@ -115,40 +116,69 @@ def tile_moe_s_lin_relu_kernel(tc, x_words, x_scales, w, offs, out):
                 )
 
         def finish(e):
-            for tile in range(e * SLOT_TILES, (e + 1) * SLOT_TILES):
-                if tile == E * SLOT_TILES - 1:
-                    nc.vector.tensor_scalar_max(results[:, tile, :], banks[tile][:], 0.0)
-                else:
-                    nc.scalar.activation(results[:, tile, :], banks[tile][:], RELU)
-                if tile in STORES:
-                    first = STORES[tile]
-                    nc.sync.dma_start(out_tiles[:, first : tile + 1, :], results[:, first : tile + 1, :])
-
-        for i, (e, g, n0, n1) in enumerate(PIECES):
-            width = n1 - n0
-            share = VECTOR_COLUMNS[i]
-            if i % 2 == 0:
-                grouped = staged[:, N - width : N, :]
-                on_scalar, on_vector = (0, width - share), (width - share, width)
+            result = results[e].rearrange("p (s n) -> p s n", s=SLOT_TILES)
+            first = e * SLOT_TILES
+            nc.scalar.activation(result[:, 0, :], banks[first][:], RELU)
+            if e < E - 1:
+                nc.scalar.activation(result[:, 1, :], banks[first + 1][:], RELU)
+                nc.sync.dma_start(out_tiles[:, first : first + SLOT_TILES, :], result)
             else:
-                grouped = staged[:, N - OVERLAP : N - OVERLAP + width, :]
-                on_scalar, on_vector = (share, width), (0, share)
-            if share < width:
-                interleave(nc.scalar.copy, grouped, raws[i], *on_scalar)
-            interleave(nc.vector.tensor_copy, grouped, raws[i], *on_vector)
-            before, after = TOKEN_STEPS[i]
-            for step in before:
-                token_step(*step)
+                nc.sync.dma_start(out_tiles[:, first, :], result[:, 0, :])
+                nc.vector.tensor_scalar_max(result[:, 1, :], banks[first + 1][:], 0.0)
+                nc.sync.dma_start(out_tiles[:, first + 1, :], result[:, 1, :])
+
+        def quantise(i):
+            e, g, n0, n1 = PIECES[i]
+            at = STAGED_AT[i]
+            if i == 1:
+                n0, at = 0, STAGED_AT[0]
             nc.vector.quantize_mx(
                 out=codes[:, e * PASSES + g, n0:n1].bitcast(FP8X4),
                 scales=scales[:, e * PASSES + g, n0:n1],
-                in_=grouped.rearrange("p n t -> p (n t)"),
+                in_=staged[:, at : at + n1 - n0, :].rearrange("p n t -> p (n t)"),
             )
-            for step in after:
-                token_step(*step)
-            if i == 2:
-                multiply(0, 0)
-            if n1 == N and i > 1:
-                multiply(e, g)
-                if g == PASSES - 1:
-                    finish(e)
+
+        def cast(i):
+            width = PIECES[i][3] - PIECES[i][2]
+            share = VECTOR_COLUMNS[i]
+            grouped = staged[:, STAGED_AT[i] : STAGED_AT[i] + width, :]
+            interleave(nc.scalar.copy, grouped, raws[i], share, width)
+            if share:
+                interleave(nc.vector.tensor_copy, grouped, raws[i], 0, share)
+
+        cast(0)
+        cast(1)
+        quantise(1)
+        token_step("words", 0, 512)
+        cast(2)
+        token_step("part", 0, 512)
+        multiply(0, 0)
+        quantise(2)
+        multiply(0, 1)
+        cast(3)
+        token_step("words", 512, 768)
+        quantise(3)
+        multiply(1, 0)
+        cast(4)
+        finish(0)
+        token_step("words", 768, 1024)
+        quantise(4)
+        multiply(1, 1)
+        cast(5)
+        token_step("part", 512, 1024)
+        quantise(5)
+        multiply(2, 0)
+        cast(6)
+        finish(1)
+        quantise(6)
+        multiply(2, 1)
+        cast(7)
+        cast(8)
+        quantise(7)
+        multiply(3, 0)
+        quantise(8)
+        cast(9)
+        finish(2)
+        quantise(9)
+        multiply(3, 1)
+        finish(3)

@@ -24,7 +24,7 @@ SLOT_TILES = C // P
 STAGED_AT = [512, 768, 0, 512, 0, 512, 0, 504, 0, 760]
 EARLY = 4
 PIECES = [(0, 0, 0, 256), (0, 0, 256, 512), (0, 1, 0, 512), (1, 0, 0, 512), (1, 1, 0, 512), (2, 0, 0, 512), (2, 1, 0, 512), (3, 0, 0, 512), (3, 1, 0, 256), (3, 1, 256, 512)]
-VECTOR_COLUMNS = [0, 0, 192, 192, 192, 192, 256, 320, 176, 176]
+VECTOR_COLUMNS = [0, 0, 128, 128, 160, 288, 320, 320, 144, 176]
 RESULT_ON = [4, 6, 9]
 
 
@@ -99,7 +99,12 @@ def tile_moe_s_lin_relu_kernel(tc, x_words, x_scales, w, offs, out):
         codes = keep.tile([P, E * PASSES, N], U32, name="codes", align_bytes=64)
         scales = keep.tile([P, E * PASSES, N], U8, name="scales", align_bytes=64)
         last = keep.tile([P, SLOT_TILES * N], F32, name="last")
-        results = [raws[i].rearrange("p j n -> p (j n)")[:, 0 : SLOT_TILES * N] for i in RESULT_ON] + [last[:]]
+        results = []
+        for i in RESULT_ON:
+            home, first = (early, 0) if i < EARLY else (late, EARLY)
+            seam = PACK * sum(n1 - n0 for e, g, n0, n1 in PIECES[first:i])
+            results.append(home[:, seam - N : seam + N] if i == len(PIECES) - 1 else home[:, seam : seam + 2 * N])
+        results.append(last[:])
         banks = [psum.tile([P, N], F32, name="bank_%d" % b) for b in range(E * SLOT_TILES)]
         out_tiles = out.rearrange("(s p) n -> p s n", p=P)
 
@@ -115,17 +120,17 @@ def tile_moe_s_lin_relu_kernel(tc, x_words, x_scales, w, offs, out):
                     stop=(g == PASSES - 1),
                 )
 
-        def finish(e):
+        def finish(e, s):
             result = results[e].rearrange("p (s n) -> p s n", s=SLOT_TILES)
-            first = e * SLOT_TILES
-            nc.scalar.activation(result[:, 0, :], banks[first][:], RELU)
-            if e < E - 1:
-                nc.scalar.activation(result[:, 1, :], banks[first + 1][:], RELU)
-                nc.sync.dma_start(out_tiles[:, first : first + SLOT_TILES, :], result)
+            tile = e * SLOT_TILES + s
+            if tile == E * SLOT_TILES - 2:
+                nc.vector.tensor_scalar_max(result[:, s, :], banks[tile][:], 0.0)
             else:
-                nc.sync.dma_start(out_tiles[:, first, :], result[:, 0, :])
-                nc.vector.tensor_scalar_max(result[:, 1, :], banks[first + 1][:], 0.0)
-                nc.sync.dma_start(out_tiles[:, first + 1, :], result[:, 1, :])
+                nc.scalar.activation(result[:, s, :], banks[tile][:], RELU)
+            if e == E - 1:
+                nc.sync.dma_start(out_tiles[:, tile, :], result[:, s, :])
+            elif s == SLOT_TILES - 1:
+                nc.sync.dma_start(out_tiles[:, tile - 1 : tile + 1, :], result)
 
         def quantise(i):
             e, g, n0, n1 = PIECES[i]
@@ -160,7 +165,8 @@ def tile_moe_s_lin_relu_kernel(tc, x_words, x_scales, w, offs, out):
         quantise(3)
         multiply(1, 0)
         cast(4)
-        finish(0)
+        finish(0, 0)
+        finish(0, 1)
         token_step("words", 768, 1024)
         quantise(4)
         multiply(1, 1)
@@ -169,16 +175,19 @@ def tile_moe_s_lin_relu_kernel(tc, x_words, x_scales, w, offs, out):
         quantise(5)
         multiply(2, 0)
         cast(6)
-        finish(1)
+        finish(1, 0)
+        finish(1, 1)
         quantise(6)
         multiply(2, 1)
         cast(7)
         cast(8)
+        finish(2, 0)
         quantise(7)
         multiply(3, 0)
         quantise(8)
         cast(9)
-        finish(2)
+        finish(2, 1)
         quantise(9)
         multiply(3, 1)
-        finish(3)
+        finish(3, 0)
+        finish(3, 1)

@@ -20,12 +20,13 @@ PACK = 4
 K_PASS = P * PACK
 PASSES = K // K_PASS
 GROUP = 16
+SLOTS = E * C
 SLOT_TILES = C // P
-STAGED_AT = [512, 768, 0, 512, 0, 512, 0, 504, 0, 760]
-EARLY = 4
-PIECES = [(0, 0, 0, 256), (0, 0, 256, 512), (0, 1, 0, 512), (1, 0, 0, 512), (1, 1, 0, 512), (2, 0, 0, 512), (2, 1, 0, 512), (3, 0, 0, 512), (3, 1, 0, 256), (3, 1, 256, 512)]
-VECTOR_COLUMNS = [0, 0, 128, 128, 160, 288, 320, 320, 144, 176]
-RESULT_ON = [4, 6, 9]
+GATHER = 512
+EARLY = 3
+PIECES = [(0, 0, 0, 512), (0, 1, 0, 512), (1, 0, 0, 512), (1, 1, 0, 512), (2, 0, 0, 512), (2, 1, 0, 512), (3, 0, 0, 512), (3, 1, 0, 256), (3, 1, 256, 512)]
+VECTOR_COLUMNS = [(0, 0), (0, 0), (256, 512), (0, 256), (256, 512), (0, 256), (256, 512), (0, 96), (0, 96)]
+STAGED_AT = [0, 512, 0, 256, 0, 256, 0, 512, 0]
 
 
 def interleave(copy, grouped, raw, c0, c1):
@@ -39,104 +40,105 @@ def tile_moe_s_lin_relu_kernel(tc, x_words, x_scales, w, offs, out):
     nc = tc.nc
     with ExitStack() as ctx:
         keep = ctx.enter_context(tc.tile_pool(name="keep", bufs=1))
+        shared = ctx.enter_context(tc.tile_pool(name="shared", bufs=1))
         psum = ctx.enter_context(tc.psum_pool(name="psum", bufs=1))
 
         raws = []
+        flats = []
 
-        def part(tile, first, i):
-            at = PACK * sum(n1 - n0 for e, g, n0, n1 in PIECES[first:i])
-            width = PIECES[i][3] - PIECES[i][2]
-            return tile[:, at : at + PACK * width].rearrange("p (j n) -> p j n", j=PACK)
-
-        def load(i, raw):
+        def load(i, tile, first):
             e, g, n0, n1 = PIECES[i]
+            at = PACK * sum(c1 - c0 for a, b, c0, c1 in PIECES[first:i])
+            flat = tile[:, at : at + PACK * (n1 - n0)]
+            raw = flat.rearrange("p (j n) -> p j n", j=PACK)
             nc.sync.dma_start(raw, w[e, g * K_PASS : (g + 1) * K_PASS, n0:n1].rearrange("(p j) n -> p j n", j=PACK))
             raws.append(raw)
+            flats.append(flat)
 
-        offsets = keep.tile([P, E * C // GROUP], U16, name="offsets")
+        offsets = keep.tile([P, SLOTS // GROUP], U16, name="offsets")
         nc.sync.dma_start(offsets[:], offs)
         early = keep.tile([P, PACK * sum(n1 - n0 for e, g, n0, n1 in PIECES[:EARLY])], F32, name="early")
-        load(0, part(early, 0, 0))
-        token_scales = keep.tile([P, T], U8, name="token_scales", tag="reused", align_bytes=64)
-        nc.vector.memset(token_scales[:].bitcast(I32), 0)
-        for q in range(4):
-            nc.sync.dma_start(
-                token_scales[32 * q : 32 * q + 4 * PASSES, :].bitcast(I32),
-                x_scales[:, 4 * q : 4 * q + 4, :].bitcast(I32),
-            )
-        load(1, part(early, 0, 1))
         token_words = keep.tile([P, T], I32, name="token_words", align_bytes=64)
         nc.sync.dma_start(token_words[:], x_words[0].rearrange("p t d -> p (t d)").bitcast(I32))
-        for i in range(2, EARLY):
-            load(i, part(early, 0, i))
+        late_words = PACK * sum(n1 - n0 for e, g, n0, n1 in PIECES[EARLY:])
+        token_scales = shared.tile([P, T], U8, name="token_scales", align_bytes=64, offset=4 * late_words - T // 2)
+        nc.vector.memset(token_scales[:].bitcast(I32), 0)
+        for r in range(4):
+            nc.sync.dma_start(
+                token_scales[r:P:16, :].bitcast(I32),
+                x_scales[:, r:16:4, :].rearrange("g q t -> q g t").bitcast(I32),
+            )
+        for i in range(EARLY):
+            load(i, early, 0)
 
-        pair_words = keep.tile([P, E * C], I32, name="pair_words", align_bytes=64)
-        slot_words = [keep.tile([P, PASSES, E * C], U8, name="slot_words_%d" % h, align_bytes=64) for h in range(2)]
-        slot_scales = [keep.tile([P, E * C], U8, name="slot_scales_%d" % g, align_bytes=64) for g in range(PASSES)]
+        pair_tile = shared.tile([P, SLOTS], I32, name="pair_words", align_bytes=64, offset=4 * late_words)
+        pair_words = [pair_tile[:, h * GATHER : (h + 1) * GATHER] for h in range(SLOTS // GATHER)]
+        slot_words = [keep.tile([P, PASSES, 2 * GATHER], U8, name="slot_words_%d" % h, align_bytes=64) for h in range(SLOTS // GATHER)]
+        slot_scales = [keep.tile([P, SLOTS], U8, name="slot_scales_%d" % g, align_bytes=64) for g in range(PASSES)]
         nc.vector.memset(slot_scales[1][:].bitcast(I32), 0)
 
-        def token_step(kind, s0, s1):
-            mine = offsets[:, s0 // GROUP : s1 // GROUP]
-            if kind == "words":
-                nc.vector.tensor_copy(pair_words[:, s0:s1].bitcast(U32), token_words[:].bitcast(U32).indirect(mine))
-            elif kind == "part":
-                nc.vector.tensor_copy(
-                    slot_words[s0 // (2 * C)][:].bitcast(U16),
-                    pair_words[:, s0:s1].bitcast(U16).rearrange("p (c g) -> p g c", g=PASSES),
-                )
-            else:
-                nc.vector.tensor_copy(slot_scales[0][:, s0:s1], token_scales[:].indirect(mine))
-                if s1 == E * C:
-                    nc.sync.dma_start(slot_scales[1][0 : 112, :].bitcast(I32), slot_scales[0][4 : 112 + 4, :].bitcast(I32))
+        def entries(h):
+            return offsets[:, h * GATHER // GROUP : (h + 1) * GATHER // GROUP]
 
-        token_step("scales", 0, 512)
-        token_step("scales", 512, 1024)
-        late = keep.tile([P, PACK * sum(n1 - n0 for e, g, n0, n1 in PIECES[EARLY:])], F32, name="late", tag="reused", align_bytes=64)
+        for h in range(SLOTS // GATHER):
+            nc.vector.tensor_copy(slot_scales[0][:, h * GATHER : (h + 1) * GATHER], token_scales[:].indirect(entries(h)))
+        nc.sync.dma_start(slot_scales[1][0:112, :].bitcast(I32), slot_scales[0][16:128, :].bitcast(I32))
+        late = shared.tile([P, late_words], F32, name="late", align_bytes=64, offset=0)
         for i in range(EARLY, len(PIECES)):
-            load(i, part(late, EARLY, i))
+            load(i, late, EARLY)
 
-        staged = keep.tile([P, 2 * N, PACK], BF16, name="staged", align_bytes=64)
+        def gather(h):
+            nc.vector.tensor_copy(pair_words[h].bitcast(U32), token_words[:].bitcast(U32).indirect(entries(h)))
+
+        def part(h):
+            nc.vector.tensor_copy(
+                slot_words[h][:].bitcast(U16),
+                pair_words[h].bitcast(U16).rearrange("p (c g) -> p g c", g=PASSES),
+            )
+
+        staged = keep.tile([P, 1024, PACK], BF16, name="staged", align_bytes=64)
         codes = keep.tile([P, E * PASSES, N], U32, name="codes", align_bytes=64)
         scales = keep.tile([P, E * PASSES, N], U8, name="scales", align_bytes=64)
-        last = keep.tile([P, SLOT_TILES * N], F32, name="last")
-        results = []
-        for i in RESULT_ON:
-            home, first = (early, 0) if i < EARLY else (late, EARLY)
-            seam = PACK * sum(n1 - n0 for e, g, n0, n1 in PIECES[first:i])
-            results.append(home[:, seam - N : seam + N] if i == len(PIECES) - 1 else home[:, seam : seam + 2 * N])
-        results.append(last[:])
+        spare = keep.tile([P, E * SLOT_TILES * N], F32, name="spare")
+        results = [spare[:, b * N : (b + 1) * N] for b in range(E * SLOT_TILES)]
+        results[4] = flats[8][:, 0:N]
+        results[5] = flats[8][:, N : 2 * N]
         banks = [psum.tile([P, N], F32, name="bank_%d" % b) for b in range(E * SLOT_TILES)]
         out_tiles = out.rearrange("(s p) n -> p s n", p=P)
 
+        def matmul(bank, tile, g, n0, n1):
+            e = tile // SLOT_TILES
+            h, first = divmod(tile * P, GATHER)
+            nc.tensor.matmul_mx(
+                out=bank,
+                lhsT=slot_words[h][:, g, 2 * first : 2 * (first + P)].bitcast(FP4X4),
+                lhsT_scale=slot_scales[g][:, tile * P : (tile + 1) * P],
+                rhs=codes[:, e * PASSES + g, n0:n1].bitcast(FP8X4),
+                rhs_scale=scales[:, e * PASSES + g, n0:n1],
+                start=(g == 0),
+                stop=(g == PASSES - 1),
+            )
+
         def multiply(e, g):
             for tile in range(e * SLOT_TILES, (e + 1) * SLOT_TILES):
-                nc.tensor.matmul_mx(
-                    out=banks[tile][:],
-                    lhsT=slot_words[tile // 4][:, g, 2 * (tile % 4) * P : 2 * (tile % 4 + 1) * P].bitcast(FP4X4),
-                    lhsT_scale=slot_scales[g][:, tile * P : (tile + 1) * P],
-                    rhs=codes[:, e * PASSES + g, :].bitcast(FP8X4),
-                    rhs_scale=scales[:, e * PASSES + g, :],
-                    start=(g == 0),
-                    stop=(g == PASSES - 1),
-                )
+                matmul(banks[tile][:], tile, g, 0, N)
 
-        def finish(e, s):
-            result = results[e].rearrange("p (s n) -> p s n", s=SLOT_TILES)
-            tile = e * SLOT_TILES + s
-            if tile == E * SLOT_TILES - 2:
-                nc.vector.tensor_scalar_max(result[:, s, :], banks[tile][:], 0.0)
+        def relu(tile, on_vector):
+            if on_vector:
+                nc.vector.tensor_scalar_max(results[tile], banks[tile][:], 0.0)
             else:
-                nc.scalar.activation(result[:, s, :], banks[tile][:], RELU)
-            if e == E - 1:
-                nc.sync.dma_start(out_tiles[:, tile, :], result[:, s, :])
-            elif s == SLOT_TILES - 1:
-                nc.sync.dma_start(out_tiles[:, tile - 1 : tile + 1, :], result)
+                nc.scalar.activation(results[tile], banks[tile][:], RELU)
 
-        def quantise(i):
+        def store(tile, count):
+            if count == 1:
+                nc.sync.dma_start(out_tiles[:, tile, :], results[tile])
+            else:
+                nc.sync.dma_start(out_tiles[:, tile : tile + count, :], spare[:, tile * N : (tile + count) * N].rearrange("p (s n) -> p s n", s=count))
+
+        def quantise(i, joined=1):
             e, g, n0, n1 = PIECES[i]
-            at = STAGED_AT[i]
-            if i == 1:
-                n0, at = 0, STAGED_AT[0]
+            n0 = PIECES[i - joined + 1][2]
+            at = STAGED_AT[i - joined + 1]
             nc.vector.quantize_mx(
                 out=codes[:, e * PASSES + g, n0:n1].bitcast(FP8X4),
                 scales=scales[:, e * PASSES + g, n0:n1],
@@ -145,49 +147,55 @@ def tile_moe_s_lin_relu_kernel(tc, x_words, x_scales, w, offs, out):
 
         def cast(i):
             width = PIECES[i][3] - PIECES[i][2]
-            share = VECTOR_COLUMNS[i]
+            v0, v1 = VECTOR_COLUMNS[i]
             grouped = staged[:, STAGED_AT[i] : STAGED_AT[i] + width, :]
-            interleave(nc.scalar.copy, grouped, raws[i], share, width)
-            if share:
-                interleave(nc.vector.tensor_copy, grouped, raws[i], 0, share)
+            if v0 > 0:
+                interleave(nc.scalar.copy, grouped, raws[i], 0, v0)
+            if v1 < width:
+                interleave(nc.scalar.copy, grouped, raws[i], v1, width)
+            if v1 > v0:
+                interleave(nc.vector.tensor_copy, grouped, raws[i], v0, v1)
 
+        gather(0)
+        gather(1)
+        part(0)
+        part(1)
         cast(0)
-        cast(1)
-        quantise(1)
-        token_step("words", 0, 512)
-        cast(2)
-        token_step("part", 0, 512)
+        quantise(0)
         multiply(0, 0)
-        quantise(2)
+        cast(1)
+        cast(2)
+        quantise(1)
         multiply(0, 1)
-        cast(3)
-        token_step("words", 512, 768)
-        quantise(3)
+        relu(0, False)
+        quantise(2)
         multiply(1, 0)
-        cast(4)
-        finish(0, 0)
-        finish(0, 1)
-        token_step("words", 768, 1024)
-        quantise(4)
+        cast(3)
+        relu(1, False)
+        quantise(3)
         multiply(1, 1)
-        cast(5)
-        token_step("part", 512, 1024)
-        quantise(5)
+        cast(4)
+        relu(2, False)
+        quantise(4)
         multiply(2, 0)
-        cast(6)
-        finish(1, 0)
-        finish(1, 1)
-        quantise(6)
+        cast(5)
+        relu(3, False)
+        store(0, 4)
+        quantise(5)
         multiply(2, 1)
+        cast(6)
         cast(7)
-        cast(8)
-        finish(2, 0)
-        quantise(7)
+        quantise(6)
         multiply(3, 0)
+        quantise(7)
+        cast(8)
+        relu(4, False)
+        store(4, 1)
+        relu(5, False)
+        store(5, 1)
         quantise(8)
-        cast(9)
-        finish(2, 1)
-        quantise(9)
         multiply(3, 1)
-        finish(3, 0)
-        finish(3, 1)
+        relu(6, True)
+        store(6, 1)
+        relu(7, False)
+        store(7, 1)

@@ -25,8 +25,8 @@ SLOT_TILES = C // P
 GATHER = 512
 EARLY = 3
 PIECES = [(0, 0, 0, 512), (0, 1, 0, 512), (1, 0, 0, 512), (1, 1, 0, 512), (2, 0, 0, 512), (2, 1, 0, 512), (3, 0, 0, 512), (3, 1, 0, 256), (3, 1, 256, 512)]
-VECTOR_COLUMNS = [(0, 0), (0, 0), (256, 512), (0, 256), (256, 512), (0, 256), (256, 512), (0, 96), (0, 96)]
-STAGED_AT = [0, 512, 0, 256, 0, 256, 0, 512, 0]
+VECTOR_COLUMNS = [(0, 0), (0, 0), (0, 256), (0, 320), (0, 320), (0, 320), (0, 288), (0, 0), (0, 160)]
+STAGED_AT = [0, 512, 1024, 1536, 2048, 2560, 3072, 3584, 3840]
 
 
 def interleave(copy, grouped, raw, c0, c1):
@@ -96,11 +96,14 @@ def tile_moe_s_lin_relu_kernel(tc, x_words, x_scales, w, offs, out):
                 pair_words[h].bitcast(U16).rearrange("p (c g) -> p g c", g=PASSES),
             )
 
-        staged = keep.tile([P, 1024, PACK], BF16, name="staged", align_bytes=64)
+        staged = keep.tile([P, 4096, PACK], BF16, name="staged", align_bytes=64)
         codes = keep.tile([P, E * PASSES, N], U32, name="codes", align_bytes=64)
         scales = keep.tile([P, E * PASSES, N], U8, name="scales", align_bytes=64)
         spare = keep.tile([P, E * SLOT_TILES * N], F32, name="spare")
         results = [spare[:, b * N : (b + 1) * N] for b in range(E * SLOT_TILES)]
+        early_results = late[:, 0 : 12 * N].rearrange("p (s n) -> p s n", s=4)[:, :, 0:N]
+        for tile in range(4):
+            results[tile] = early_results[:, tile, :]
         results[4] = flats[8][:, 0:N]
         results[5] = flats[8][:, N : 2 * N]
         banks = [psum.tile([P, N], F32, name="bank_%d" % b) for b in range(E * SLOT_TILES)]
@@ -167,10 +170,10 @@ def tile_moe_s_lin_relu_kernel(tc, x_words, x_scales, w, offs, out):
         cast(2)
         quantise(1)
         multiply(0, 1)
-        relu(0, False)
         quantise(2)
         multiply(1, 0)
         cast(3)
+        relu(0, False)
         relu(1, False)
         quantise(3)
         multiply(1, 1)
@@ -180,15 +183,15 @@ def tile_moe_s_lin_relu_kernel(tc, x_words, x_scales, w, offs, out):
         multiply(2, 0)
         cast(5)
         relu(3, False)
-        store(0, 4)
+        nc.sync.dma_start(out_tiles[:, 0:4, :], early_results)
         quantise(5)
         multiply(2, 1)
         cast(6)
-        cast(7)
         quantise(6)
         multiply(3, 0)
-        quantise(7)
+        cast(7)
         cast(8)
+        quantise(7)
         relu(4, False)
         store(4, 1)
         relu(5, False)

@@ -109,7 +109,7 @@ def tile_moe_s_lin_relu_kernel(tc, x_words, x_scales, w, offs, out):
         banks = [psum.tile([P, N], F32, name="bank_%d" % b) for b in range(E * SLOT_TILES)]
         out_tiles = out.rearrange("(s p) n -> p s n", p=P)
 
-        def matmul(bank, tile, g, n0, n1):
+        def matmul(bank, tile, g, n0, n1, opens):
             e = tile // SLOT_TILES
             h, first = divmod(tile * P, GATHER)
             nc.tensor.matmul_mx(
@@ -118,13 +118,13 @@ def tile_moe_s_lin_relu_kernel(tc, x_words, x_scales, w, offs, out):
                 lhsT_scale=slot_scales[g][:, tile * P : (tile + 1) * P],
                 rhs=codes[:, e * PASSES + g, n0:n1].bitcast(FP8X4),
                 rhs_scale=scales[:, e * PASSES + g, n0:n1],
-                start=(g == 0),
-                stop=(g == PASSES - 1),
+                start=opens,
+                stop=not opens,
             )
 
         def multiply(e, g):
             for tile in range(e * SLOT_TILES, (e + 1) * SLOT_TILES):
-                matmul(banks[tile][:], tile, g, 0, N)
+                matmul(banks[tile][:], tile, g, 0, N, g == 0)
 
         def relu(tile, on_vector):
             if on_vector:
@@ -180,25 +180,29 @@ def tile_moe_s_lin_relu_kernel(tc, x_words, x_scales, w, offs, out):
         cast(4)
         relu(2, False)
         quantise(4)
-        multiply(2, 0)
+        matmul(banks[4][:], 4, 0, 0, N, True)
         cast(5)
         relu(3, False)
         nc.sync.dma_start(out_tiles[:, 0:4, :], early_results)
         quantise(5)
-        multiply(2, 1)
+        matmul(banks[4][:], 4, 1, 0, N, False)
+        matmul(banks[5][:], 5, 1, 0, N, True)
+        matmul(banks[5][:], 5, 0, 0, N, False)
         cast(6)
+        fourth = raws[6][:, 0:2, 0:256]
+        nc.vector.tensor_scalar_max(fourth, banks[4][:].rearrange("p (j n) -> p j n", j=2), 0.0)
+        nc.sync.dma_start(out_tiles[:, 4, :].rearrange("p (j n) -> p j n", j=2), fourth)
         quantise(6)
         multiply(3, 0)
         cast(7)
         cast(8)
         quantise(7)
-        relu(4, False)
-        store(4, 1)
         relu(5, False)
         store(5, 1)
         quantise(8)
         multiply(3, 1)
-        relu(6, True)
-        store(6, 1)
+        for n0 in (0, 256):
+            nc.vector.tensor_scalar_max(results[6][:, n0 : n0 + 256], banks[6][:, n0 : n0 + 256], 0.0)
+            nc.sync.dma_start(out_tiles[:, 6, n0 : n0 + 256], results[6][:, n0 : n0 + 256])
         relu(7, False)
         store(7, 1)

@@ -19,19 +19,23 @@ P = 128
 PACK = 4
 K_PASS = P * PACK
 PASSES = K // K_PASS
-GROUP = 16
 SLOTS = E * C
-SLOT_TILES = C // P
+SLOT_TILES = SLOTS // P
+TILES_AN_EXPERT = C // P
+GROUP = 16
 GATHER = 512
+SCALE_ROWS = 4
+PASS_1_ABOVE = 16
+HALF = N // 2
+
+PIECES = [(e, g, 0, N) for e in range(E) for g in range(PASSES)][:-1] + [(E - 1, 1, 0, HALF), (E - 1, 1, HALF, N)]
 EARLY = 3
-PIECES = [(0, 0, 0, 512), (0, 1, 0, 512), (1, 0, 0, 512), (1, 1, 0, 512), (2, 0, 0, 512), (2, 1, 0, 512), (3, 0, 0, 512), (3, 1, 0, 256), (3, 1, 256, 512)]
-VECTOR_COLUMNS = [(0, 0), (0, 0), (0, 256), (0, 320), (0, 320), (0, 320), (0, 288), (0, 0), (0, 160)]
-STAGED_AT = [0, 512, 1024, 1536, 2048, 2560, 3072, 3584, 3840]
+VECTOR_COLUMNS = [0, 0, 256, 320, 320, 320, 288, 0, 160]
 
 
-def interleave(copy, grouped, raw, c0, c1):
+def round_and_interleave(copy, staged, raw, c0, c1):
     copy(
-        out=grouped[:, c0:c1, :].rearrange("p (c i) t -> p c t i", i=4),
+        out=staged[:, c0:c1, :].rearrange("p (c i) t -> p c t i", i=4),
         in_=raw[:, :, c0:c1].rearrange("p t (c i) -> p c t i", i=4),
     )
 
@@ -44,35 +48,35 @@ def tile_moe_s_lin_relu_kernel(tc, x_words, x_scales, w, offs, out):
         psum = ctx.enter_context(tc.psum_pool(name="psum", bufs=1))
 
         raws = []
-        flats = []
 
-        def load(i, tile, first):
+        def floats(pieces):
+            return PACK * sum(n1 - n0 for e, g, n0, n1 in pieces)
+
+        def load(i, home, first):
             e, g, n0, n1 = PIECES[i]
-            at = PACK * sum(c1 - c0 for a, b, c0, c1 in PIECES[first:i])
-            flat = tile[:, at : at + PACK * (n1 - n0)]
-            raw = flat.rearrange("p (j n) -> p j n", j=PACK)
-            nc.sync.dma_start(raw, w[e, g * K_PASS : (g + 1) * K_PASS, n0:n1].rearrange("(p j) n -> p j n", j=PACK))
+            at = floats(PIECES[first:i])
+            raw = home[:, at : at + PACK * (n1 - n0)].rearrange("p (t n) -> p t n", t=PACK)
+            nc.sync.dma_start(raw, w[e, g * K_PASS : (g + 1) * K_PASS, n0:n1].rearrange("(p t) n -> p t n", t=PACK))
             raws.append(raw)
-            flats.append(flat)
 
         offsets = keep.tile([P, SLOTS // GROUP], U16, name="offsets")
         nc.sync.dma_start(offsets[:], offs)
-        early = keep.tile([P, PACK * sum(n1 - n0 for e, g, n0, n1 in PIECES[:EARLY])], F32, name="early")
+        early = keep.tile([P, floats(PIECES[:EARLY])], F32, name="early")
         token_words = keep.tile([P, T], I32, name="token_words", align_bytes=64)
         nc.sync.dma_start(token_words[:], x_words[0].rearrange("p t d -> p (t d)").bitcast(I32))
-        late_words = PACK * sum(n1 - n0 for e, g, n0, n1 in PIECES[EARLY:])
-        token_scales = shared.tile([P, T], U8, name="token_scales", align_bytes=64, offset=4 * late_words - T // 2)
+
+        late_bytes = 4 * floats(PIECES[EARLY:])
+        token_scales = shared.tile([P, T], U8, name="token_scales", align_bytes=64, offset=late_bytes - T // 2)
         nc.vector.memset(token_scales[:].bitcast(I32), 0)
-        for r in range(4):
+        for r in range(SCALE_ROWS):
             nc.sync.dma_start(
-                token_scales[r:P:16, :].bitcast(I32),
-                x_scales[:, r:16:4, :].rearrange("g q t -> q g t").bitcast(I32),
+                token_scales[r:P:PASS_1_ABOVE, :].bitcast(I32),
+                x_scales[:, r::SCALE_ROWS, :].rearrange("g q t -> q g t").bitcast(I32),
             )
         for i in range(EARLY):
             load(i, early, 0)
 
-        pair_tile = shared.tile([P, SLOTS], I32, name="pair_words", align_bytes=64, offset=4 * late_words)
-        pair_words = [pair_tile[:, h * GATHER : (h + 1) * GATHER] for h in range(SLOTS // GATHER)]
+        pair_words = shared.tile([P, SLOTS], I32, name="pair_words", align_bytes=64, offset=late_bytes)
         slot_words = [keep.tile([P, PASSES, 2 * GATHER], U8, name="slot_words_%d" % h, align_bytes=64) for h in range(SLOTS // GATHER)]
         slot_scales = [keep.tile([P, SLOTS], U8, name="slot_scales_%d" % g, align_bytes=64) for g in range(PASSES)]
         nc.vector.memset(slot_scales[1][:].bitcast(I32), 0)
@@ -82,127 +86,132 @@ def tile_moe_s_lin_relu_kernel(tc, x_words, x_scales, w, offs, out):
 
         for h in range(SLOTS // GATHER):
             nc.vector.tensor_copy(slot_scales[0][:, h * GATHER : (h + 1) * GATHER], token_scales[:].indirect(entries(h)))
-        nc.sync.dma_start(slot_scales[1][0:112, :].bitcast(I32), slot_scales[0][16:128, :].bitcast(I32))
-        late = shared.tile([P, late_words], F32, name="late", align_bytes=64, offset=0)
+        nc.sync.dma_start(slot_scales[1][0 : P - PASS_1_ABOVE, :].bitcast(I32), slot_scales[0][PASS_1_ABOVE:P, :].bitcast(I32))
+        late = shared.tile([P, late_bytes // 4], F32, name="late", align_bytes=64, offset=0)
         for i in range(EARLY, len(PIECES)):
             load(i, late, EARLY)
 
-        def gather(h):
-            nc.vector.tensor_copy(pair_words[h].bitcast(U32), token_words[:].bitcast(U32).indirect(entries(h)))
-
-        def part(h):
-            nc.vector.tensor_copy(
-                slot_words[h][:].bitcast(U16),
-                pair_words[h].bitcast(U16).rearrange("p (c g) -> p g c", g=PASSES),
-            )
-
-        staged = keep.tile([P, 4096, PACK], BF16, name="staged", align_bytes=64)
+        staged = keep.tile([P, E * PASSES * N, PACK], BF16, name="staged", align_bytes=64)
         codes = keep.tile([P, E * PASSES, N], U32, name="codes", align_bytes=64)
         scales = keep.tile([P, E * PASSES, N], U8, name="scales", align_bytes=64)
-        spare = keep.tile([P, E * SLOT_TILES * N], F32, name="spare")
-        results = [spare[:, b * N : (b + 1) * N] for b in range(E * SLOT_TILES)]
-        early_results = late[:, 0 : 12 * N].rearrange("p (s n) -> p s n", s=4)[:, :, 0:N]
-        for tile in range(4):
-            results[tile] = early_results[:, tile, :]
-        results[4] = flats[8][:, 0:N]
-        results[5] = flats[8][:, N : 2 * N]
-        banks = [psum.tile([P, N], F32, name="bank_%d" % b) for b in range(E * SLOT_TILES)]
+        last_results = keep.tile([P, TILES_AN_EXPERT * N], F32, name="last_results")
+        banks = [psum.tile([P, N], F32, name="bank_%d" % tile) for tile in range(SLOT_TILES)]
         out_tiles = out.rearrange("(s p) n -> p s n", p=P)
 
-        def matmul(bank, tile, g, n0, n1, opens):
-            e = tile // SLOT_TILES
-            h, first = divmod(tile * P, GATHER)
-            nc.tensor.matmul_mx(
-                out=bank,
-                lhsT=slot_words[h][:, g, 2 * first : 2 * (first + P)].bitcast(FP4X4),
-                lhsT_scale=slot_scales[g][:, tile * P : (tile + 1) * P],
-                rhs=codes[:, e * PASSES + g, n0:n1].bitcast(FP8X4),
-                rhs_scale=scales[:, e * PASSES + g, n0:n1],
-                start=opens,
-                stop=not opens,
+        first_results = late[:, 0 : 4 * 3 * N].rearrange("p (s n) -> p s n", s=4)[:, :, 0:N]
+        result_4 = raws[6][:, 0:2, 0:HALF]
+        result_5 = raws[8][:, 2:4, :].rearrange("p t n -> p (t n)")
+        result_6 = last_results[:, 0:N]
+        result_7 = last_results[:, N : 2 * N]
+
+        def gather_words(h):
+            nc.vector.tensor_copy(
+                pair_words[:, h * GATHER : (h + 1) * GATHER].bitcast(U32), token_words[:].bitcast(U32).indirect(entries(h))
             )
 
-        def multiply(e, g):
-            for tile in range(e * SLOT_TILES, (e + 1) * SLOT_TILES):
-                matmul(banks[tile][:], tile, g, 0, N, g == 0)
+        def part_passes(h):
+            nc.vector.tensor_copy(
+                slot_words[h][:].bitcast(U16),
+                pair_words[:, h * GATHER : (h + 1) * GATHER].bitcast(U16).rearrange("p (c g) -> p g c", g=PASSES),
+            )
 
-        def relu(tile, on_vector):
-            if on_vector:
-                nc.vector.tensor_scalar_max(results[tile], banks[tile][:], 0.0)
-            else:
-                nc.scalar.activation(results[tile], banks[tile][:], RELU)
-
-        def store(tile, count):
-            if count == 1:
-                nc.sync.dma_start(out_tiles[:, tile, :], results[tile])
-            else:
-                nc.sync.dma_start(out_tiles[:, tile : tile + count, :], spare[:, tile * N : (tile + count) * N].rearrange("p (s n) -> p s n", s=count))
-
-        def quantise(i, joined=1):
+        def staging(i):
             e, g, n0, n1 = PIECES[i]
-            n0 = PIECES[i - joined + 1][2]
-            at = STAGED_AT[i - joined + 1]
+            block = (e * PASSES + g) * N
+            return staged[:, block + n0 : block + n1, :]
+
+        def round_piece(i):
+            width = PIECES[i][3] - PIECES[i][2]
+            share = VECTOR_COLUMNS[i]
+            round_and_interleave(nc.scalar.copy, staging(i), raws[i], share, width)
+            if share:
+                round_and_interleave(nc.vector.tensor_copy, staging(i), raws[i], 0, share)
+
+        def quantise(i):
+            e, g, n0, n1 = PIECES[i]
             nc.vector.quantize_mx(
                 out=codes[:, e * PASSES + g, n0:n1].bitcast(FP8X4),
                 scales=scales[:, e * PASSES + g, n0:n1],
-                in_=staged[:, at : at + n1 - n0, :].rearrange("p n t -> p (n t)"),
+                in_=staging(i).rearrange("p n t -> p (n t)"),
             )
 
-        def cast(i):
-            width = PIECES[i][3] - PIECES[i][2]
-            v0, v1 = VECTOR_COLUMNS[i]
-            grouped = staged[:, STAGED_AT[i] : STAGED_AT[i] + width, :]
-            if v0 > 0:
-                interleave(nc.scalar.copy, grouped, raws[i], 0, v0)
-            if v1 < width:
-                interleave(nc.scalar.copy, grouped, raws[i], v1, width)
-            if v1 > v0:
-                interleave(nc.vector.tensor_copy, grouped, raws[i], v0, v1)
+        def multiply(tile, g, n0, n1, opens, closes):
+            block = tile // TILES_AN_EXPERT * PASSES + g
+            h, first = divmod(tile * P, GATHER)
+            nc.tensor.matmul_mx(
+                out=banks[tile][:, n0:n1],
+                lhsT=slot_words[h][:, g, 2 * first : 2 * (first + P)].bitcast(FP4X4),
+                lhsT_scale=slot_scales[g][:, tile * P : (tile + 1) * P],
+                rhs=codes[:, block, n0:n1].bitcast(FP8X4),
+                rhs_scale=scales[:, block, n0:n1],
+                start=opens,
+                stop=closes,
+            )
 
-        gather(0)
-        gather(1)
-        part(0)
-        part(1)
-        cast(0)
+        def multiply_expert(e, g):
+            for tile in range(e * TILES_AN_EXPERT, (e + 1) * TILES_AN_EXPERT):
+                multiply(tile, g, 0, N, g == 0, g == 1)
+
+        def multiply_last_pass(piece):
+            e, g, n0, n1 = PIECES[piece]
+            for tile in range(e * TILES_AN_EXPERT, (e + 1) * TILES_AN_EXPERT):
+                for c0 in range(n0, n1, P):
+                    multiply(tile, g, c0, c0 + P, False, c0 + P == N)
+
+        def relu_on_scalar(result, bank):
+            nc.scalar.activation(result, bank, RELU)
+
+        def relu_on_vector(result, bank):
+            nc.vector.tensor_scalar_max(result, bank, 0.0)
+
+        for h in range(SLOTS // GATHER):
+            gather_words(h)
+        for h in range(SLOTS // GATHER):
+            part_passes(h)
+
+        round_piece(0)
         quantise(0)
-        multiply(0, 0)
-        cast(1)
-        cast(2)
+        multiply_expert(0, 0)
+        round_piece(1)
+        round_piece(2)
         quantise(1)
-        multiply(0, 1)
+        multiply_expert(0, 1)
         quantise(2)
-        multiply(1, 0)
-        cast(3)
-        relu(0, False)
-        relu(1, False)
+        multiply_expert(1, 0)
+        round_piece(3)
+        relu_on_scalar(first_results[:, 0, :], banks[0][:])
+        relu_on_scalar(first_results[:, 1, :], banks[1][:])
         quantise(3)
-        multiply(1, 1)
-        cast(4)
-        relu(2, False)
+        multiply_expert(1, 1)
+
+        round_piece(4)
+        relu_on_scalar(first_results[:, 2, :], banks[2][:])
         quantise(4)
-        matmul(banks[4][:], 4, 0, 0, N, True)
-        cast(5)
-        relu(3, False)
-        nc.sync.dma_start(out_tiles[:, 0:4, :], early_results)
+        multiply(4, 0, 0, N, True, False)
+        round_piece(5)
+        relu_on_scalar(first_results[:, 3, :], banks[3][:])
+        nc.sync.dma_start(out_tiles[:, 0:4, :], first_results)
         quantise(5)
-        matmul(banks[4][:], 4, 1, 0, N, False)
-        matmul(banks[5][:], 5, 1, 0, N, True)
-        matmul(banks[5][:], 5, 0, 0, N, False)
-        cast(6)
-        fourth = raws[6][:, 0:2, 0:256]
-        nc.vector.tensor_scalar_max(fourth, banks[4][:].rearrange("p (j n) -> p j n", j=2), 0.0)
-        nc.sync.dma_start(out_tiles[:, 4, :].rearrange("p (j n) -> p j n", j=2), fourth)
+        multiply(4, 1, 0, N, False, True)
+        multiply(5, 1, 0, N, True, False)
+        multiply(5, 0, 0, N, False, True)
+
+        round_piece(6)
+        relu_on_vector(result_4, banks[4][:].rearrange("p (j n) -> p j n", j=2))
+        nc.sync.dma_start(out_tiles[:, 4, :].rearrange("p (j n) -> p j n", j=2), result_4)
         quantise(6)
-        multiply(3, 0)
-        cast(7)
-        cast(8)
+        multiply_expert(3, 0)
+        round_piece(7)
+        round_piece(8)
         quantise(7)
-        relu(5, False)
-        store(5, 1)
+        multiply_last_pass(7)
+        relu_on_scalar(result_5, banks[5][:])
+        nc.sync.dma_start(out_tiles[:, 5, :], result_5)
         quantise(8)
-        multiply(3, 1)
-        for n0 in (0, 256):
-            nc.vector.tensor_scalar_max(results[6][:, n0 : n0 + 256], banks[6][:, n0 : n0 + 256], 0.0)
-            nc.sync.dma_start(out_tiles[:, 6, n0 : n0 + 256], results[6][:, n0 : n0 + 256])
-        relu(7, False)
-        store(7, 1)
+        multiply_last_pass(8)
+
+        for n0 in (0, HALF):
+            relu_on_vector(result_6[:, n0 : n0 + HALF], banks[6][:, n0 : n0 + HALF])
+            nc.sync.dma_start(out_tiles[:, 6, n0 : n0 + HALF], result_6[:, n0 : n0 + HALF])
+        relu_on_scalar(result_7, banks[7][:])
+        nc.sync.dma_start(out_tiles[:, 7, :], result_7)

@@ -28,9 +28,9 @@ SCALE_ROWS = 4
 PASS_1_ABOVE = 16
 HALF = N // 2
 
-PIECES = [(e, g, 0, N) for e in range(E) for g in range(PASSES)][:-1] + [(E - 1, 1, 0, HALF), (E - 1, 1, HALF, N)]
+PIECES = [(e, g, 0, N) for e in range(E - 1) for g in range(PASSES)] + [(E - 1, g, n0, n0 + HALF) for n0 in (0, HALF) for g in range(PASSES)]
 EARLY = 3
-VECTOR_COLUMNS = [0, 0, 256, 320, 320, 320, 288, 0, 160]
+VECTOR_COLUMNS = [0, 0, 256, 320, 320, 320, 0, 256, 0, 160]
 
 
 def round_and_interleave(copy, staged, raw, c0, c1):
@@ -94,15 +94,14 @@ def tile_moe_s_lin_relu_kernel(tc, x_words, x_scales, w, offs, out):
         staged = keep.tile([P, E * PASSES * N, PACK], BF16, name="staged", align_bytes=64)
         codes = keep.tile([P, E * PASSES, N], U32, name="codes", align_bytes=64)
         scales = keep.tile([P, E * PASSES, N], U8, name="scales", align_bytes=64)
-        last_results = keep.tile([P, TILES_AN_EXPERT * N], F32, name="last_results")
+        last_results = keep.tile([P, TILES_AN_EXPERT * HALF], F32, name="last_results")
         banks = [psum.tile([P, N], F32, name="bank_%d" % tile) for tile in range(SLOT_TILES)]
         out_tiles = out.rearrange("(s p) n -> p s n", p=P)
 
-        first_results = late[:, 0 : 4 * 3 * N].rearrange("p (s n) -> p s n", s=4)[:, :, 0:N]
-        result_4 = raws[6][:, 0:2, 0:HALF]
-        result_5 = raws[8][:, 2:4, :].rearrange("p t n -> p (t n)")
-        result_6 = last_results[:, 0:N]
-        result_7 = last_results[:, N : 2 * N]
+        first_results = late[:, 0 : 4 * 2 * N].rearrange("p (s n) -> p s n", s=4)[:, :, 0:N]
+        middle_results = late[:, floats(PIECES[EARLY:6]) : floats(PIECES[EARLY:8])].rearrange("p (s n) -> p s n", s=2)[:, :, 0:N]
+        low_results = raws[9][:, 0:2, :]
+        high_results = last_results[:].rearrange("p (s n) -> p s n", s=2)
 
         def gather_words(h):
             nc.vector.tensor_copy(
@@ -123,7 +122,8 @@ def tile_moe_s_lin_relu_kernel(tc, x_words, x_scales, w, offs, out):
         def round_piece(i):
             width = PIECES[i][3] - PIECES[i][2]
             share = VECTOR_COLUMNS[i]
-            round_and_interleave(nc.scalar.copy, staging(i), raws[i], share, width)
+            if share < width:
+                round_and_interleave(nc.scalar.copy, staging(i), raws[i], share, width)
             if share:
                 round_and_interleave(nc.vector.tensor_copy, staging(i), raws[i], 0, share)
 
@@ -135,11 +135,11 @@ def tile_moe_s_lin_relu_kernel(tc, x_words, x_scales, w, offs, out):
                 in_=staging(i).rearrange("p n t -> p (n t)"),
             )
 
-        def multiply(tile, g, n0, n1, opens, closes):
+        def multiply(sums, tile, g, n0, n1, opens, closes):
             block = tile // TILES_AN_EXPERT * PASSES + g
             h, first = divmod(tile * P, GATHER)
             nc.tensor.matmul_mx(
-                out=banks[tile][:, n0:n1],
+                out=sums,
                 lhsT=slot_words[h][:, g, 2 * first : 2 * (first + P)].bitcast(FP4X4),
                 lhsT_scale=slot_scales[g][:, tile * P : (tile + 1) * P],
                 rhs=codes[:, block, n0:n1].bitcast(FP8X4),
@@ -150,13 +150,20 @@ def tile_moe_s_lin_relu_kernel(tc, x_words, x_scales, w, offs, out):
 
         def multiply_expert(e, g):
             for tile in range(e * TILES_AN_EXPERT, (e + 1) * TILES_AN_EXPERT):
-                multiply(tile, g, 0, N, g == 0, g == 1)
+                multiply(banks[tile][:], tile, g, 0, N, g == 0, g == 1)
 
-        def multiply_last_pass(piece):
-            e, g, n0, n1 = PIECES[piece]
-            for tile in range(e * TILES_AN_EXPERT, (e + 1) * TILES_AN_EXPERT):
-                for c0 in range(n0, n1, P):
-                    multiply(tile, g, c0, c0 + P, False, c0 + P == N)
+        def multiply_low(g):
+            for j in range(2):
+                for c0 in (0, P):
+                    at = j * HALF + c0
+                    multiply(banks[6][:, at : at + P], 6 + j, g, c0, c0 + P, g == 0 and at == 0, g == 1 and at == N - P)
+
+        high_banks = [banks[7], banks[0]]
+
+        def multiply_high(g):
+            for j in range(2):
+                for c0 in (0, P):
+                    multiply(high_banks[j][:, c0 : c0 + P], 6 + j, g, HALF + c0, HALF + c0 + P, g == 0 and c0 == 0, g == 1 and c0 == P)
 
         def relu_on_scalar(result, bank):
             nc.scalar.activation(result, bank, RELU)
@@ -186,32 +193,32 @@ def tile_moe_s_lin_relu_kernel(tc, x_words, x_scales, w, offs, out):
 
         round_piece(4)
         relu_on_scalar(first_results[:, 2, :], banks[2][:])
-        quantise(4)
-        multiply(4, 0, 0, N, True, False)
-        round_piece(5)
         relu_on_scalar(first_results[:, 3, :], banks[3][:])
         nc.sync.dma_start(out_tiles[:, 0:4, :], first_results)
+        quantise(4)
+        multiply_expert(2, 0)
+        round_piece(5)
         quantise(5)
-        multiply(4, 1, 0, N, False, True)
-        multiply(5, 1, 0, N, True, False)
-        multiply(5, 0, 0, N, False, True)
+        multiply_expert(2, 1)
 
         round_piece(6)
-        relu_on_vector(result_4, banks[4][:].rearrange("p (j n) -> p j n", j=2))
-        nc.sync.dma_start(out_tiles[:, 4, :].rearrange("p (j n) -> p j n", j=2), result_4)
-        quantise(6)
-        multiply_expert(3, 0)
+        relu_on_scalar(middle_results[:, 0, :], banks[4][:])
         round_piece(7)
-        round_piece(8)
+        quantise(6)
+        multiply_low(0)
         quantise(7)
-        multiply_last_pass(7)
-        relu_on_scalar(result_5, banks[5][:])
-        nc.sync.dma_start(out_tiles[:, 5, :], result_5)
+        multiply_low(1)
+        relu_on_vector(middle_results[:, 1, :], banks[5][:])
+        nc.sync.dma_start(out_tiles[:, 4:6, :], middle_results)
+        round_piece(8)
+        round_piece(9)
         quantise(8)
-        multiply_last_pass(8)
-
-        for n0 in (0, HALF):
-            relu_on_vector(result_6[:, n0 : n0 + HALF], banks[6][:, n0 : n0 + HALF])
-            nc.sync.dma_start(out_tiles[:, 6, n0 : n0 + HALF], result_6[:, n0 : n0 + HALF])
-        relu_on_scalar(result_7, banks[7][:])
-        nc.sync.dma_start(out_tiles[:, 7, :], result_7)
+        multiply_high(0)
+        quantise(9)
+        relu_on_scalar(low_results, banks[6][:].rearrange("p (s n) -> p s n", s=2))
+        nc.sync.dma_start(out_tiles[:, 6:8, 0:HALF], low_results)
+        multiply_high(1)
+        relu_on_vector(high_results[:, 0, :], high_banks[0][:, 0:HALF])
+        nc.sync.dma_start(out_tiles[:, 6, HALF:N], high_results[:, 0, :])
+        relu_on_scalar(high_results[:, 1, :], high_banks[1][:, 0:HALF])
+        nc.sync.dma_start(out_tiles[:, 7, HALF:N], high_results[:, 1, :])

@@ -28,9 +28,13 @@ SCALE_ROWS = 4
 PASS_1_ABOVE = 16
 HALF = N // 2
 
-PIECES = [(e, g, 0, N) for e in range(E - 1) for g in range(PASSES)] + [(E - 1, g, n0, n0 + HALF) for n0 in (0, HALF) for g in range(PASSES)]
+PIECES = (
+    [(e, g, 0, N) for e in range(E - 1) for g in range(PASSES)][:-1]
+    + [(2, 1, n0, n0 + HALF) for n0 in (0, HALF)]
+    + [(3, g, n0, n0 + HALF) for n0 in (0, HALF) for g in range(PASSES)]
+)
 EARLY = 3
-VECTOR_COLUMNS = [0, 0, 256, 320, 320, 320, 0, 256, 0, 160]
+VECTOR_COLUMNS = [0, 0, 256, 320, 320, 0, 256, 0, 256, 0, 160]
 
 
 def round_and_interleave(copy, staged, raw, c0, c1):
@@ -99,8 +103,8 @@ def tile_moe_s_lin_relu_kernel(tc, x_words, x_scales, w, offs, out):
         out_tiles = out.rearrange("(s p) n -> p s n", p=P)
 
         first_results = late[:, 0 : 4 * 2 * N].rearrange("p (s n) -> p s n", s=4)[:, :, 0:N]
-        middle_results = late[:, floats(PIECES[EARLY:6]) : floats(PIECES[EARLY:8])].rearrange("p (s n) -> p s n", s=2)[:, :, 0:N]
-        low_results = raws[9][:, 0:2, :]
+        middle_results = late[:, floats(PIECES[EARLY:7]) : floats(PIECES[EARLY:9])].rearrange("p (s n) -> p s n", s=2)[:, :, 0:N]
+        low_results = raws[10][:, 0:2, :]
         high_results = last_results[:].rearrange("p (s n) -> p s n", s=2)
 
         def gather_words(h):
@@ -152,6 +156,12 @@ def tile_moe_s_lin_relu_kernel(tc, x_words, x_scales, w, offs, out):
             for tile in range(e * TILES_AN_EXPERT, (e + 1) * TILES_AN_EXPERT):
                 multiply(banks[tile][:], tile, g, 0, N, g == 0, g == 1)
 
+        def multiply_half(piece, closes):
+            e, g, n0, n1 = PIECES[piece]
+            for tile in range(e * TILES_AN_EXPERT, (e + 1) * TILES_AN_EXPERT):
+                for c0 in range(n0, n1, P):
+                    multiply(banks[tile][:, c0 : c0 + P], tile, g, c0, c0 + P, False, closes and c0 + P == n1)
+
         def multiply_low(g):
             for j in range(2):
                 for c0 in (0, P):
@@ -193,28 +203,31 @@ def tile_moe_s_lin_relu_kernel(tc, x_words, x_scales, w, offs, out):
 
         round_piece(4)
         relu_on_scalar(first_results[:, 2, :], banks[2][:])
-        relu_on_scalar(first_results[:, 3, :], banks[3][:])
-        nc.sync.dma_start(out_tiles[:, 0:4, :], first_results)
         quantise(4)
         multiply_expert(2, 0)
+        relu_on_vector(first_results[:, 3, :], banks[3][:])
+        nc.sync.dma_start(out_tiles[:, 0:4, :], first_results)
         round_piece(5)
-        quantise(5)
-        multiply_expert(2, 1)
-
         round_piece(6)
-        relu_on_scalar(middle_results[:, 0, :], banks[4][:])
-        round_piece(7)
+        quantise(5)
+        multiply_half(5, False)
         quantise(6)
-        multiply_low(0)
+        multiply_half(6, True)
+
+        round_piece(7)
+        relu_on_scalar(middle_results[:, 0, :], banks[4][:])
+        round_piece(8)
         quantise(7)
+        multiply_low(0)
+        quantise(8)
         multiply_low(1)
         relu_on_vector(middle_results[:, 1, :], banks[5][:])
         nc.sync.dma_start(out_tiles[:, 4:6, :], middle_results)
-        round_piece(8)
         round_piece(9)
-        quantise(8)
-        multiply_high(0)
+        round_piece(10)
         quantise(9)
+        multiply_high(0)
+        quantise(10)
         relu_on_scalar(low_results, banks[6][:].rearrange("p (s n) -> p s n", s=2))
         nc.sync.dma_start(out_tiles[:, 6:8, 0:HALF], low_results)
         multiply_high(1)

@@ -34,7 +34,7 @@ PIECES = (
     + [(3, g, n0, n0 + HALF) for n0 in (0, HALF) for g in range(PASSES)]
 )
 EARLY = 3
-VECTOR_COLUMNS = [0, 0, 256, 320, 320, 0, 256, 0, 256, 0, 160]
+VECTOR_COLUMNS = [0, 0, 256, 352, 320, 0, 256, 0, 256, 0, 160]
 
 
 def round_and_interleave(copy, staged, raw, c0, c1):
@@ -98,14 +98,13 @@ def tile_moe_s_lin_relu_kernel(tc, x_words, x_scales, w, offs, out):
         staged = keep.tile([P, E * PASSES * N, PACK], BF16, name="staged", align_bytes=64)
         codes = keep.tile([P, E * PASSES, N], U32, name="codes", align_bytes=64)
         scales = keep.tile([P, E * PASSES, N], U8, name="scales", align_bytes=64)
-        last_results = keep.tile([P, TILES_AN_EXPERT * HALF], F32, name="last_results")
+        high_results = keep.tile([P, TILES_AN_EXPERT, HALF], F32, name="high_results")
         banks = [psum.tile([P, N], F32, name="bank_%d" % tile) for tile in range(SLOT_TILES)]
         out_tiles = out.rearrange("(s p) n -> p s n", p=P)
 
         first_results = late[:, 0 : 4 * 2 * N].rearrange("p (s n) -> p s n", s=4)[:, :, 0:N]
         middle_results = late[:, floats(PIECES[EARLY:7]) : floats(PIECES[EARLY:9])].rearrange("p (s n) -> p s n", s=2)[:, :, 0:N]
         low_results = raws[10][:, 0:2, :]
-        high_results = last_results[:].rearrange("p (s n) -> p s n", s=2)
 
         def gather_words(h):
             nc.vector.tensor_copy(
@@ -158,12 +157,12 @@ def tile_moe_s_lin_relu_kernel(tc, x_words, x_scales, w, offs, out):
 
         def multiply_half(piece, closes):
             e, g, n0, n1 = PIECES[piece]
-            for tile in range(e * TILES_AN_EXPERT, (e + 1) * TILES_AN_EXPERT):
-                for c0 in range(n0, n1, P):
-                    multiply(banks[tile][:, c0 : c0 + P], tile, g, c0, c0 + P, False, closes and c0 + P == n1)
+            tile = e * TILES_AN_EXPERT
+            for c0 in range(n0, n1, P):
+                multiply(banks[tile][:, c0 : c0 + P], tile, g, c0, c0 + P, False, closes and c0 + P == n1)
 
         def multiply_low(g):
-            for j in range(2):
+            for j in range(TILES_AN_EXPERT):
                 for c0 in (0, P):
                     at = j * HALF + c0
                     multiply(banks[6][:, at : at + P], 6 + j, g, c0, c0 + P, g == 0 and at == 0, g == 1 and at == N - P)
@@ -171,7 +170,7 @@ def tile_moe_s_lin_relu_kernel(tc, x_words, x_scales, w, offs, out):
         high_banks = [banks[7], banks[0]]
 
         def multiply_high(g):
-            for j in range(2):
+            for j in range(TILES_AN_EXPERT):
                 for c0 in (0, P):
                     multiply(high_banks[j][:, c0 : c0 + P], 6 + j, g, HALF + c0, HALF + c0 + P, g == 0 and c0 == 0, g == 1 and c0 == P)
 
@@ -204,7 +203,7 @@ def tile_moe_s_lin_relu_kernel(tc, x_words, x_scales, w, offs, out):
         round_piece(4)
         relu_on_scalar(first_results[:, 2, :], banks[2][:])
         quantise(4)
-        multiply_expert(2, 0)
+        multiply(banks[4][:], 4, 0, 0, N, True, False)
         relu_on_vector(first_results[:, 3, :], banks[3][:])
         nc.sync.dma_start(out_tiles[:, 0:4, :], first_results)
         round_piece(5)
@@ -213,6 +212,8 @@ def tile_moe_s_lin_relu_kernel(tc, x_words, x_scales, w, offs, out):
         multiply_half(5, False)
         quantise(6)
         multiply_half(6, True)
+        multiply(banks[5][:], 5, 1, 0, N, True, False)
+        multiply(banks[5][:], 5, 0, 0, N, False, True)
 
         round_piece(7)
         relu_on_scalar(middle_results[:, 0, :], banks[4][:])
@@ -231,6 +232,7 @@ def tile_moe_s_lin_relu_kernel(tc, x_words, x_scales, w, offs, out):
         relu_on_scalar(low_results, banks[6][:].rearrange("p (s n) -> p s n", s=2))
         nc.sync.dma_start(out_tiles[:, 6:8, 0:HALF], low_results)
         multiply_high(1)
+
         relu_on_vector(high_results[:, 0, :], high_banks[0][:, 0:HALF])
         nc.sync.dma_start(out_tiles[:, 6, HALF:N], high_results[:, 0, :])
         relu_on_scalar(high_results[:, 1, :], high_banks[1][:, 0:HALF])

@@ -130,13 +130,16 @@ def tile_moe_s_lin_relu_kernel(tc, x_words, x_scales, w, offs, out):
             if share:
                 round_and_interleave(nc.vector.tensor_copy, staging(i), raws[i], 0, share)
 
-        def quantise(i):
+        def quantise_columns(i, c0, c1):
             e, g, n0, n1 = PIECES[i]
             nc.vector.quantize_mx(
-                out=codes[:, e * PASSES + g, n0:n1].bitcast(FP8X4),
-                scales=scales[:, e * PASSES + g, n0:n1],
-                in_=staging(i).rearrange("p n t -> p (n t)"),
+                out=codes[:, e * PASSES + g, n0 + c0 : n0 + c1].bitcast(FP8X4),
+                scales=scales[:, e * PASSES + g, n0 + c0 : n0 + c1],
+                in_=staging(i)[:, c0:c1, :].rearrange("p n t -> p (n t)"),
             )
+
+        def quantise(i):
+            quantise_columns(i, 0, PIECES[i][3] - PIECES[i][2])
 
         def multiply(sums, tile, g, n0, n1, opens, closes):
             block = tile // TILES_AN_EXPERT * PASSES + g
@@ -167,12 +170,11 @@ def tile_moe_s_lin_relu_kernel(tc, x_words, x_scales, w, offs, out):
                     at = j * HALF + c0
                     multiply(banks[6][:, at : at + P], 6 + j, g, c0, c0 + P, g == 0 and at == 0, g == 1 and at == N - P)
 
-        high_banks = [banks[7], banks[0]]
+        high_banks = {0: [banks[7], banks[0]], P: [banks[1], banks[2]]}
 
-        def multiply_high(g):
+        def multiply_high(g, c0):
             for j in range(TILES_AN_EXPERT):
-                for c0 in (0, P):
-                    multiply(high_banks[j][:, c0 : c0 + P], 6 + j, g, HALF + c0, HALF + c0 + P, g == 0 and c0 == 0, g == 1 and c0 == P)
+                multiply(high_banks[c0][j][:, 0:P], 6 + j, g, HALF + c0, HALF + c0 + P, g == 0, g == 1)
 
         def relu_on_scalar(result, bank):
             nc.scalar.activation(result, bank, RELU)
@@ -227,13 +229,16 @@ def tile_moe_s_lin_relu_kernel(tc, x_words, x_scales, w, offs, out):
         round_piece(9)
         round_piece(10)
         quantise(9)
-        multiply_high(0)
-        quantise(10)
+        multiply_high(0, 0)
+        multiply_high(0, P)
+        quantise_columns(10, 0, P)
+        multiply_high(1, 0)
+        quantise_columns(10, P, HALF)
         relu_on_scalar(low_results, banks[6][:].rearrange("p (s n) -> p s n", s=2))
         nc.sync.dma_start(out_tiles[:, 6:8, 0:HALF], low_results)
-        multiply_high(1)
+        multiply_high(1, P)
 
-        relu_on_vector(high_results[:, 0, :], high_banks[0][:, 0:HALF])
-        nc.sync.dma_start(out_tiles[:, 6, HALF:N], high_results[:, 0, :])
-        relu_on_scalar(high_results[:, 1, :], high_banks[1][:, 0:HALF])
-        nc.sync.dma_start(out_tiles[:, 7, HALF:N], high_results[:, 1, :])
+        for part, c0 in enumerate((0, P)):
+            relu_on_vector(high_results[:, part, 0:P], high_banks[c0][0][:, 0:P])
+            relu_on_scalar(high_results[:, part, P:HALF], high_banks[c0][1][:, 0:P])
+            nc.sync.dma_start(out_tiles[:, 6:8, HALF + c0 : HALF + c0 + P], high_results[:, part, :].rearrange("p (s n) -> p s n", s=2))

@@ -34,7 +34,7 @@ PIECES = (
     + [(3, g, n0, n0 + HALF) for n0 in (0, HALF) for g in range(PASSES)]
 )
 EARLY = 3
-VECTOR_COLUMNS = [0, 0, 256, 352, 320, 0, 256, 0, 256, 0, 160]
+VECTOR_COLUMNS = [0, 0, 304, 288, 320, 0, 256, 0, 256, 0, 160]
 
 
 def round_and_interleave(copy, staged, raw, c0, c1):
@@ -102,7 +102,7 @@ def tile_moe_s_lin_relu_kernel(tc, x_words, x_scales, w, offs, out):
         banks = [psum.tile([P, N], F32, name="bank_%d" % tile) for tile in range(SLOT_TILES)]
         out_tiles = out.rearrange("(s p) n -> p s n", p=P)
 
-        first_results = late[:, 0 : 4 * 2 * N].rearrange("p (s n) -> p s n", s=4)[:, :, 0:N]
+        first_results = late[:, 0 : 4 * 1280].rearrange("p (s n) -> p s n", s=4)[:, :, 0:N]
         middle_results = late[:, floats(PIECES[EARLY:7]) : floats(PIECES[EARLY:9])].rearrange("p (s n) -> p s n", s=2)[:, :, 0:N]
         low_results = raws[10][:, 0:2, :]
 
@@ -203,19 +203,19 @@ def tile_moe_s_lin_relu_kernel(tc, x_words, x_scales, w, offs, out):
         multiply_expert(1, 1)
 
         round_piece(4)
-        relu_on_scalar(first_results[:, 2, :], banks[2][:])
         quantise(4)
         multiply(banks[4][:], 4, 0, 0, N, True, False)
-        relu_on_vector(first_results[:, 3, :], banks[3][:])
-        nc.sync.dma_start(out_tiles[:, 0:4, :], first_results)
+        multiply(banks[5][:], 5, 0, 0, N, True, False)
+        relu_on_vector(first_results[:, 2, :], banks[2][:])
         round_piece(5)
+        relu_on_scalar(first_results[:, 3, :], banks[3][:])
+        nc.sync.dma_start(out_tiles[:, 0:4, :], first_results)
         round_piece(6)
         quantise(5)
         multiply_half(5, False)
         quantise(6)
         multiply_half(6, True)
-        multiply(banks[5][:], 5, 1, 0, N, True, False)
-        multiply(banks[5][:], 5, 0, 0, N, False, True)
+        multiply(banks[5][:], 5, 1, 0, N, False, True)
 
         round_piece(7)
         relu_on_scalar(middle_results[:, 0, :], banks[4][:])

@@ -27,6 +27,7 @@ GATHER = 512
 SCALE_ROWS = 4
 PASS_1_ABOVE = 16
 HALF = N // 2
+LEAD = 112
 
 PIECES = (
     [(e, g, 0, N) for e in range(E - 1) for g in range(PASSES)][:-1]
@@ -34,7 +35,8 @@ PIECES = (
     + [(3, g, n0, n0 + HALF) for n0 in (0, HALF) for g in range(PASSES)]
 )
 EARLY = 3
-VECTOR_COLUMNS = [0, 0, 304, 288, 320, 0, 256, 0, 256, 0, 160]
+VECTOR_COLUMNS = [0, 0, 304, 288, 320, 0, 256, 0, 256, 192, 192]
+SCALAR_CUTS = {3: N - LEAD, 5: 144}
 
 
 def round_and_interleave(copy, staged, raw, c0, c1):
@@ -69,7 +71,7 @@ def tile_moe_s_lin_relu_kernel(tc, x_words, x_scales, w, offs, out):
         token_words = keep.tile([P, T], I32, name="token_words", align_bytes=64)
         nc.sync.dma_start(token_words[:], x_words[0].rearrange("p t d -> p (t d)").bitcast(I32))
 
-        late_bytes = 4 * floats(PIECES[EARLY:])
+        late_bytes = 4 * (LEAD + floats(PIECES[EARLY:]))
         token_scales = shared.tile([P, T], U8, name="token_scales", align_bytes=64, offset=late_bytes - T // 2)
         nc.vector.memset(token_scales[:].bitcast(I32), 0)
         for r in range(SCALE_ROWS):
@@ -93,7 +95,7 @@ def tile_moe_s_lin_relu_kernel(tc, x_words, x_scales, w, offs, out):
         nc.sync.dma_start(slot_scales[1][0 : P - PASS_1_ABOVE, :].bitcast(I32), slot_scales[0][PASS_1_ABOVE:P, :].bitcast(I32))
         late = shared.tile([P, late_bytes // 4], F32, name="late", align_bytes=64, offset=0)
         for i in range(EARLY, len(PIECES)):
-            load(i, late, EARLY)
+            load(i, late[:, LEAD:], EARLY)
 
         staged = keep.tile([P, E * PASSES * N, PACK], BF16, name="staged", align_bytes=64)
         codes = keep.tile([P, E * PASSES, N], U32, name="codes", align_bytes=64)
@@ -103,8 +105,8 @@ def tile_moe_s_lin_relu_kernel(tc, x_words, x_scales, w, offs, out):
         out_tiles = out.rearrange("(s p) n -> p s n", p=P)
 
         first_results = late[:, 0 : 4 * 1280].rearrange("p (s n) -> p s n", s=4)[:, :, 0:N]
-        middle_results = late[:, floats(PIECES[EARLY:7]) : floats(PIECES[EARLY:9])].rearrange("p (s n) -> p s n", s=2)[:, :, 0:N]
-        low_results = raws[10][:, 0:2, :]
+        middle_results = raws[6].rearrange("p (s t) n -> p s (t n)", s=2)
+        low_results = raws[8][:, 0:2, :]
 
         def gather_words(h):
             nc.vector.tensor_copy(
@@ -125,8 +127,11 @@ def tile_moe_s_lin_relu_kernel(tc, x_words, x_scales, w, offs, out):
         def round_piece(i):
             width = PIECES[i][3] - PIECES[i][2]
             share = VECTOR_COLUMNS[i]
-            if share < width:
-                round_and_interleave(nc.scalar.copy, staging(i), raws[i], share, width)
+            cut = SCALAR_CUTS.get(i, width)
+            if share < cut:
+                round_and_interleave(nc.scalar.copy, staging(i), raws[i], share, cut)
+            if cut < width:
+                round_and_interleave(nc.scalar.copy, staging(i), raws[i], cut, width)
             if share:
                 round_and_interleave(nc.vector.tensor_copy, staging(i), raws[i], 0, share)
 
@@ -219,23 +224,25 @@ def tile_moe_s_lin_relu_kernel(tc, x_words, x_scales, w, offs, out):
 
         round_piece(7)
         relu_on_scalar(middle_results[:, 0, :], banks[4][:])
+        relu_on_scalar(middle_results[:, 1, :], banks[5][:])
+        nc.sync.dma_start(out_tiles[:, 4:6, :], middle_results)
         round_piece(8)
         quantise(7)
         multiply_low(0)
         quantise(8)
         multiply_low(1)
-        relu_on_vector(middle_results[:, 1, :], banks[5][:])
-        nc.sync.dma_start(out_tiles[:, 4:6, :], middle_results)
         round_piece(9)
-        round_piece(10)
+        relu_on_scalar(low_results, banks[6][:].rearrange("p (s n) -> p s n", s=2))
+        nc.sync.dma_start(out_tiles[:, 6:8, 0:HALF], low_results)
         quantise(9)
         multiply_high(0, 0)
         multiply_high(0, P)
+        round_and_interleave(nc.scalar.copy, staging(10), raws[10], VECTOR_COLUMNS[10], HALF)
+        round_and_interleave(nc.vector.tensor_copy, staging(10), raws[10], 0, P)
+        round_and_interleave(nc.vector.tensor_copy, staging(10), raws[10], P, VECTOR_COLUMNS[10])
         quantise_columns(10, 0, P)
         multiply_high(1, 0)
         quantise_columns(10, P, HALF)
-        relu_on_scalar(low_results, banks[6][:].rearrange("p (s n) -> p s n", s=2))
-        nc.sync.dma_start(out_tiles[:, 6:8, 0:HALF], low_results)
         multiply_high(1, P)
 
         for part, c0 in enumerate((0, P)):

@@ -105,8 +105,9 @@ def tile_moe_s_lin_relu_kernel(tc, x_words, x_scales, w, offs, out):
         out_tiles = out.rearrange("(s p) n -> p s n", p=P)
 
         first_results = late[:, 0 : 4 * 1280].rearrange("p (s n) -> p s n", s=4)[:, :, 0:N]
-        middle_results = raws[6].rearrange("p (s t) n -> p s (t n)", s=2)
-        low_results = raws[8][:, 0:2, :]
+        middle_at = LEAD + floats(PIECES[EARLY:6])
+        middle_results = late[:, middle_at : middle_at + 4 * N].rearrange("p (s n) -> p s n", s=2)[:, :, 0:N]
+        low_results = raws[8][:, 0:PACK:2, :]
 
         def gather_words(h):
             nc.vector.tensor_copy(
@@ -245,7 +246,7 @@ def tile_moe_s_lin_relu_kernel(tc, x_words, x_scales, w, offs, out):
         quantise_columns(10, P, HALF)
         multiply_high(1, P)
 
-        for part, c0 in enumerate((0, P)):
-            relu_on_vector(high_results[:, part, 0:P], high_banks[c0][0][:, 0:P])
-            relu_on_scalar(high_results[:, part, P:HALF], high_banks[c0][1][:, 0:P])
-            nc.sync.dma_start(out_tiles[:, 6:8, HALF + c0 : HALF + c0 + P], high_results[:, part, :].rearrange("p (s n) -> p s n", s=2))
+        for c0 in (0, P):
+            relu_on_vector(high_results[:, 0, c0 : c0 + P], high_banks[c0][0][:, 0:P])
+            relu_on_scalar(high_results[:, 1, c0 : c0 + P], high_banks[c0][1][:, 0:P])
+            nc.sync.dma_start(out_tiles[:, 6:8, HALF + c0 : HALF + c0 + P], high_results[:, :, c0 : c0 + P])

@@ -27,7 +27,8 @@ GATHER = 512
 SCALE_ROWS = 4
 PASS_1_ABOVE = 16
 HALF = N // 2
-LEAD = 112
+AXI = 256
+LEAD = 128
 
 PIECES = (
     [(e, g, 0, N) for e in range(E - 1) for g in range(PASSES)][:-1]
@@ -36,7 +37,7 @@ PIECES = (
 )
 EARLY = 3
 VECTOR_COLUMNS = [0, 0, 304, 288, 320, 0, 256, 0, 256, 192, 192]
-SCALAR_CUTS = {3: N - LEAD, 5: 144}
+SCALAR_CUTS = {3: N - LEAD, 5: LEAD}
 
 
 def round_and_interleave(copy, staged, raw, c0, c1):
@@ -65,14 +66,14 @@ def tile_moe_s_lin_relu_kernel(tc, x_words, x_scales, w, offs, out):
             nc.sync.dma_start(raw, w[e, g * K_PASS : (g + 1) * K_PASS, n0:n1].rearrange("(p t) n -> p t n", t=PACK))
             raws.append(raw)
 
-        offsets = keep.tile([P, SLOTS // GROUP], U16, name="offsets")
+        offsets = keep.tile([P, SLOTS // GROUP], U16, name="offsets", align_bytes=AXI)
         nc.sync.dma_start(offsets[:], offs)
-        early = keep.tile([P, floats(PIECES[:EARLY])], F32, name="early")
-        token_words = keep.tile([P, T], I32, name="token_words", align_bytes=64)
+        early = keep.tile([P, floats(PIECES[:EARLY])], F32, name="early", align_bytes=AXI)
+        token_words = keep.tile([P, T], I32, name="token_words", align_bytes=AXI)
         nc.sync.dma_start(token_words[:], x_words[0].rearrange("p t d -> p (t d)").bitcast(I32))
 
         late_bytes = 4 * (LEAD + floats(PIECES[EARLY:]))
-        token_scales = shared.tile([P, T], U8, name="token_scales", align_bytes=64, offset=late_bytes - T // 2)
+        token_scales = shared.tile([P, T], U8, name="token_scales", align_bytes=AXI, offset=late_bytes - T // 2)
         nc.vector.memset(token_scales[:].bitcast(I32), 0)
         for r in range(SCALE_ROWS):
             nc.sync.dma_start(
@@ -82,9 +83,9 @@ def tile_moe_s_lin_relu_kernel(tc, x_words, x_scales, w, offs, out):
         for i in range(EARLY):
             load(i, early, 0)
 
-        pair_words = shared.tile([P, SLOTS], I32, name="pair_words", align_bytes=64, offset=late_bytes)
+        pair_words = shared.tile([P, SLOTS], I32, name="pair_words", align_bytes=AXI, offset=late_bytes)
         slot_words = [keep.tile([P, PASSES, 2 * GATHER], U8, name="slot_words_%d" % h, align_bytes=64) for h in range(SLOTS // GATHER)]
-        slot_scales = [keep.tile([P, SLOTS], U8, name="slot_scales_%d" % g, align_bytes=64) for g in range(PASSES)]
+        slot_scales = [keep.tile([P, SLOTS], U8, name="slot_scales_%d" % g, align_bytes=AXI) for g in range(PASSES)]
         nc.vector.memset(slot_scales[1][:].bitcast(I32), 0)
 
         def entries(h):
@@ -93,14 +94,14 @@ def tile_moe_s_lin_relu_kernel(tc, x_words, x_scales, w, offs, out):
         for h in range(SLOTS // GATHER):
             nc.vector.tensor_copy(slot_scales[0][:, h * GATHER : (h + 1) * GATHER], token_scales[:].indirect(entries(h)))
         nc.sync.dma_start(slot_scales[1][0 : P - PASS_1_ABOVE, :].bitcast(I32), slot_scales[0][PASS_1_ABOVE:P, :].bitcast(I32))
-        late = shared.tile([P, late_bytes // 4], F32, name="late", align_bytes=64, offset=0)
+        late = shared.tile([P, late_bytes // 4], F32, name="late", align_bytes=AXI, offset=0)
         for i in range(EARLY, len(PIECES)):
             load(i, late[:, LEAD:], EARLY)
 
         staged = keep.tile([P, E * PASSES * N, PACK], BF16, name="staged", align_bytes=64)
         codes = keep.tile([P, E * PASSES, N], U32, name="codes", align_bytes=64)
         scales = keep.tile([P, E * PASSES, N], U8, name="scales", align_bytes=64)
-        high_results = keep.tile([P, TILES_AN_EXPERT, HALF], F32, name="high_results")
+        high_results = keep.tile([P, TILES_AN_EXPERT, HALF], F32, name="high_results", align_bytes=AXI)
         banks = [psum.tile([P, N], F32, name="bank_%d" % tile) for tile in range(SLOT_TILES)]
         out_tiles = out.rearrange("(s p) n -> p s n", p=P)
 

@@ -31,13 +31,12 @@ AXI = 256
 LEAD = 128
 
 PIECES = (
-    [(e, g, 0, N) for e in range(E - 1) for g in range(PASSES)][:-1]
-    + [(2, 1, n0, n0 + HALF) for n0 in (0, HALF)]
+    [(e, g, 0, N) for e in range(E - 1) for g in range(PASSES)]
     + [(3, g, n0, n0 + HALF) for n0 in (0, HALF) for g in range(PASSES)]
 )
 EARLY = 3
-VECTOR_COLUMNS = [0, 0, 304, 288, 320, 0, 256, 0, 256, 192, 192]
-SCALAR_CUTS = {3: N - LEAD, 5: LEAD}
+VECTOR_COLUMNS = [0, 0, 304, 288, 320, 288, 0, 256, 192, 192]
+SCALAR_CUTS = {3: N - LEAD}
 
 
 def round_and_interleave(copy, staged, raw, c0, c1):
@@ -93,7 +92,8 @@ def tile_moe_s_lin_relu_kernel(tc, x_words, x_scales, w, offs, out):
 
         for h in range(SLOTS // GATHER):
             nc.vector.tensor_copy(slot_scales[0][:, h * GATHER : (h + 1) * GATHER], token_scales[:].indirect(entries(h)))
-        nc.sync.dma_start(slot_scales[1][0 : P - PASS_1_ABOVE, :].bitcast(I32), slot_scales[0][PASS_1_ABOVE:P, :].bitcast(I32))
+        for r in range(SCALE_ROWS):
+            nc.sync.dma_start(slot_scales[1][r:P:32, :].bitcast(I32), slot_scales[0][PASS_1_ABOVE + r : P : 32, :].bitcast(I32))
         late = shared.tile([P, late_bytes // 4], F32, name="late", align_bytes=AXI, offset=0)
         for i in range(EARLY, len(PIECES)):
             load(i, late[:, LEAD:], EARLY)
@@ -105,10 +105,9 @@ def tile_moe_s_lin_relu_kernel(tc, x_words, x_scales, w, offs, out):
         banks = [psum.tile([P, N], F32, name="bank_%d" % tile) for tile in range(SLOT_TILES)]
         out_tiles = out.rearrange("(s p) n -> p s n", p=P)
 
-        first_results = late[:, 0 : 4 * 1280].rearrange("p (s n) -> p s n", s=4)[:, :, 0:N]
-        middle_at = LEAD + floats(PIECES[EARLY:6])
-        middle_results = late[:, middle_at : middle_at + 4 * N].rearrange("p (s n) -> p s n", s=2)[:, :, 0:N]
-        low_results = raws[8][:, 0:PACK:2, :]
+        first_results = late[:, 0 : 8 * N].rearrange("p (s n) -> p s n", s=4)[:, :, 0:N]
+        middle_results = raws[5][:, 0:PACK:2, :]
+        low_results = raws[7][:, 0:PACK:2, :]
 
         def gather_words(h):
             nc.vector.tensor_copy(
@@ -165,12 +164,6 @@ def tile_moe_s_lin_relu_kernel(tc, x_words, x_scales, w, offs, out):
             for tile in range(e * TILES_AN_EXPERT, (e + 1) * TILES_AN_EXPERT):
                 multiply(banks[tile][:], tile, g, 0, N, g == 0, g == 1)
 
-        def multiply_half(piece, closes):
-            e, g, n0, n1 = PIECES[piece]
-            tile = e * TILES_AN_EXPERT
-            for c0 in range(n0, n1, P):
-                multiply(banks[tile][:, c0 : c0 + P], tile, g, c0, c0 + P, False, closes and c0 + P == n1)
-
         def multiply_low(g):
             for j in range(TILES_AN_EXPERT):
                 for c0 in (0, P):
@@ -210,44 +203,43 @@ def tile_moe_s_lin_relu_kernel(tc, x_words, x_scales, w, offs, out):
         multiply_expert(1, 1)
 
         round_piece(4)
-        quantise(4)
-        multiply(banks[4][:], 4, 0, 0, N, True, False)
-        multiply(banks[5][:], 5, 0, 0, N, True, False)
-        relu_on_vector(first_results[:, 2, :], banks[2][:])
-        round_piece(5)
         relu_on_scalar(first_results[:, 3, :], banks[3][:])
+        quantise(4)
+        multiply_expert(2, 0)
+        relu_on_vector(first_results[:, 2, :], banks[2][:])
         nc.sync.dma_start(out_tiles[:, 0:4, :], first_results)
-        round_piece(6)
-        quantise(5)
-        multiply_half(5, False)
-        quantise(6)
-        multiply_half(6, True)
+        round_and_interleave(nc.scalar.copy, staging(5), raws[5], VECTOR_COLUMNS[5], N)
+        round_and_interleave(nc.vector.tensor_copy, staging(5), raws[5], 0, HALF)
+        round_and_interleave(nc.vector.tensor_copy, staging(5), raws[5], HALF, VECTOR_COLUMNS[5])
+        for n0 in (0, HALF):
+            quantise_columns(5, n0, n0 + HALF)
+            multiply(banks[4][:, n0 : n0 + HALF], 4, 1, n0, n0 + HALF, False, n0 == HALF)
         multiply(banks[5][:], 5, 1, 0, N, False, True)
 
-        round_piece(7)
+        round_piece(6)
         relu_on_scalar(middle_results[:, 0, :], banks[4][:])
         relu_on_scalar(middle_results[:, 1, :], banks[5][:])
         nc.sync.dma_start(out_tiles[:, 4:6, :], middle_results)
-        round_piece(8)
-        quantise(7)
+        round_piece(7)
+        quantise(6)
         multiply_low(0)
-        quantise(8)
+        quantise(7)
         multiply_low(1)
-        round_piece(9)
+        round_piece(8)
         relu_on_scalar(low_results, banks[6][:].rearrange("p (s n) -> p s n", s=2))
         nc.sync.dma_start(out_tiles[:, 6:8, 0:HALF], low_results)
-        quantise(9)
+        quantise(8)
         multiply_high(0, 0)
         multiply_high(0, P)
-        round_and_interleave(nc.scalar.copy, staging(10), raws[10], VECTOR_COLUMNS[10], HALF)
-        round_and_interleave(nc.vector.tensor_copy, staging(10), raws[10], 0, P)
-        round_and_interleave(nc.vector.tensor_copy, staging(10), raws[10], P, VECTOR_COLUMNS[10])
-        quantise_columns(10, 0, P)
+        round_and_interleave(nc.scalar.copy, staging(9), raws[9], VECTOR_COLUMNS[9], HALF)
+        round_and_interleave(nc.vector.tensor_copy, staging(9), raws[9], 0, P)
+        round_and_interleave(nc.vector.tensor_copy, staging(9), raws[9], P, VECTOR_COLUMNS[9])
+        quantise_columns(9, 0, P)
         multiply_high(1, 0)
-        quantise_columns(10, P, HALF)
+        quantise_columns(9, P, HALF)
         multiply_high(1, P)
 
         for c0 in (0, P):
             relu_on_vector(high_results[:, 0, c0 : c0 + P], high_banks[c0][0][:, 0:P])
             relu_on_scalar(high_results[:, 1, c0 : c0 + P], high_banks[c0][1][:, 0:P])
-            nc.sync.dma_start(out_tiles[:, 6:8, HALF + c0 : HALF + c0 + P], high_results[:, :, c0 : c0 + P])
+        nc.sync.dma_start(out_tiles[:, 6:8, HALF:N], high_results[:])

@@ -41,8 +41,8 @@ SCALAR_CUTS = {3: N - LEAD}
 
 def round_and_interleave(copy, staged, raw, c0, c1):
     copy(
-        out=staged[:, c0:c1, :].rearrange("p (c i) t -> p c t i", i=4),
-        in_=raw[:, :, c0:c1].rearrange("p t (c i) -> p c t i", i=4),
+        out=staged[:, c0:c1, :].rearrange("p (c i) t -> p c t i", i=2),
+        in_=raw[:, :, c0:c1].rearrange("p t (c i) -> p c t i", i=2),
     )
 
 
@@ -65,11 +65,11 @@ def tile_moe_s_lin_relu_kernel(tc, x_words, x_scales, w, offs, out):
             nc.sync.dma_start(raw, w[e, g * K_PASS : (g + 1) * K_PASS, n0:n1].rearrange("(p t) n -> p t n", t=PACK))
             raws.append(raw)
 
-        offsets = keep.tile([P, SLOTS // GROUP], U16, name="offsets", align_bytes=AXI)
-        nc.sync.dma_start(offsets[:], offs)
         early = keep.tile([P, floats(PIECES[:EARLY])], F32, name="early", align_bytes=AXI)
         token_words = keep.tile([P, T], I32, name="token_words", align_bytes=AXI)
         nc.sync.dma_start(token_words[:], x_words[0].rearrange("p t d -> p (t d)").bitcast(I32))
+        offsets = keep.tile([P, SLOTS // GROUP], U16, name="offsets", align_bytes=AXI)
+        nc.sync.dma_start(offsets[:], offs)
 
         late_bytes = 4 * (LEAD + floats(PIECES[EARLY:]))
         token_scales = shared.tile([P, T], U8, name="token_scales", align_bytes=AXI, offset=late_bytes - T // 2)

@@ -23,9 +23,9 @@ SLOTS = E * C
 SLOT_TILES = SLOTS // P
 TILES_AN_EXPERT = C // P
 GROUP = 16
-GATHER = 512
+SPARE = 512
 SCALE_ROWS = 4
-PASS_1_ABOVE = 16
+QUADRANT = 32
 HALF = N // 2
 AXI = 256
 LEAD = 128
@@ -34,9 +34,9 @@ PIECES = (
     [(e, g, 0, N) for e in range(E - 1) for g in range(PASSES)]
     + [(3, g, n0, n0 + HALF) for n0 in (0, HALF) for g in range(PASSES)]
 )
-EARLY = 3
-VECTOR_COLUMNS = [0, 0, 304, 288, 320, 288, 0, 256, 192, 192]
-SCALAR_CUTS = {3: N - LEAD}
+EARLY = 4
+VECTOR_COLUMNS = [0, 0, 0, 0, 320, 320, 0, 256, 192, 192]
+SCALAR_CUTS = {4: N - LEAD}
 
 
 def round_and_interleave(copy, staged, raw, c0, c1):
@@ -50,7 +50,6 @@ def tile_moe_s_lin_relu_kernel(tc, x_words, x_scales, w, offs, out):
     nc = tc.nc
     with ExitStack() as ctx:
         keep = ctx.enter_context(tc.tile_pool(name="keep", bufs=1))
-        shared = ctx.enter_context(tc.tile_pool(name="shared", bufs=1))
         psum = ctx.enter_context(tc.psum_pool(name="psum", bufs=1))
 
         raws = []
@@ -65,38 +64,35 @@ def tile_moe_s_lin_relu_kernel(tc, x_words, x_scales, w, offs, out):
             nc.sync.dma_start(raw, w[e, g * K_PASS : (g + 1) * K_PASS, n0:n1].rearrange("(p t) n -> p t n", t=PACK))
             raws.append(raw)
 
-        early = keep.tile([P, floats(PIECES[:EARLY])], F32, name="early", align_bytes=AXI)
-        token_words = keep.tile([P, T], I32, name="token_words", align_bytes=AXI)
-        nc.sync.dma_start(token_words[:], x_words[0].rearrange("p t d -> p (t d)").bitcast(I32))
+        token_words = keep.tile([P, T + SPARE], I32, name="token_words", align_bytes=AXI)
+        nc.sync.dma_start(token_words[:, 0:T], x_words[0].rearrange("p t d -> p (t d)").bitcast(I32))
         offsets = keep.tile([P, SLOTS // GROUP], U16, name="offsets", align_bytes=AXI)
         nc.sync.dma_start(offsets[:], offs)
 
-        late_bytes = 4 * (LEAD + floats(PIECES[EARLY:]))
-        token_scales = shared.tile([P, T], U8, name="token_scales", align_bytes=AXI, offset=late_bytes - T // 2)
-        nc.vector.memset(token_scales[:].bitcast(I32), 0)
+        token_scales = keep.tile([P, PASSES * T + SPARE], U8, name="token_scales", align_bytes=AXI)
+        nc.vector.memset(token_scales[:, 0 : PASSES * T].bitcast(I32), 0)
         for r in range(SCALE_ROWS):
             nc.sync.dma_start(
-                token_scales[r:P:PASS_1_ABOVE, :].bitcast(I32),
+                token_scales[r:P:QUADRANT, 0 : PASSES * T].bitcast(I32).rearrange("q (g t) -> q g t", g=PASSES),
                 x_scales[:, r::SCALE_ROWS, :].rearrange("g q t -> q g t").bitcast(I32),
             )
+        nc.vector.memset(token_scales[:, PASSES * T :].bitcast(I32), 0)
+        nc.vector.memset(token_words[:, T:], 0)
+
+        early = keep.tile([P, floats(PIECES[:EARLY])], F32, name="early", align_bytes=AXI)
         for i in range(EARLY):
             load(i, early, 0)
-
-        pair_words = shared.tile([P, SLOTS], I32, name="pair_words", align_bytes=AXI, offset=late_bytes)
-        slot_words = [keep.tile([P, PASSES, 2 * GATHER], U8, name="slot_words_%d" % h, align_bytes=64) for h in range(SLOTS // GATHER)]
-        slot_scales = [keep.tile([P, SLOTS], U8, name="slot_scales_%d" % g, align_bytes=AXI) for g in range(PASSES)]
-        nc.vector.memset(slot_scales[1][:].bitcast(I32), 0)
-
-        def entries(h):
-            return offsets[:, h * GATHER // GROUP : (h + 1) * GATHER // GROUP]
-
-        for h in range(SLOTS // GATHER):
-            nc.vector.tensor_copy(slot_scales[0][:, h * GATHER : (h + 1) * GATHER], token_scales[:].indirect(entries(h)))
-        for r in range(SCALE_ROWS):
-            nc.sync.dma_start(slot_scales[1][r:P:32, :].bitcast(I32), slot_scales[0][PASS_1_ABOVE + r : P : 32, :].bitcast(I32))
-        late = shared.tile([P, late_bytes // 4], F32, name="late", align_bytes=AXI, offset=0)
+        late = keep.tile([P, LEAD + floats(PIECES[EARLY:])], F32, name="late", align_bytes=AXI)
         for i in range(EARLY, len(PIECES)):
             load(i, late[:, LEAD:], EARLY)
+
+        pair_words = keep.tile([P, SLOTS], I32, name="pair_words", align_bytes=64)
+        slot_words = keep.tile([P, PASSES, 2 * SLOTS], U8, name="slot_words", align_bytes=64)
+        slot_scales = [keep.tile([P, SLOTS], U8, name="slot_scales_%d" % g, align_bytes=64) for g in range(PASSES)]
+        nc.vector.tensor_copy(pair_words[:].bitcast(U32), token_words[:].bitcast(U32).indirect(offsets[:]))
+        for g in range(PASSES):
+            nc.vector.tensor_copy(slot_scales[g][:], token_scales[:, g * T : (g + 1) * T + SPARE].indirect(offsets[:]))
+        nc.vector.tensor_copy(slot_words[:].bitcast(U16), pair_words[:].bitcast(U16).rearrange("p (c g) -> p g c", g=PASSES))
 
         staged = keep.tile([P, E * PASSES * N, PACK], BF16, name="staged", align_bytes=64)
         codes = keep.tile([P, E * PASSES, N], U32, name="codes", align_bytes=64)
@@ -106,19 +102,8 @@ def tile_moe_s_lin_relu_kernel(tc, x_words, x_scales, w, offs, out):
         out_tiles = out.rearrange("(s p) n -> p s n", p=P)
 
         first_results = late[:, 0 : 8 * N].rearrange("p (s n) -> p s n", s=4)[:, :, 0:N]
-        middle_results = raws[5][:, 0:PACK:2, :]
+        middle_results = raws[0][:, 0:PACK:2, :]
         low_results = raws[7][:, 0:PACK:2, :]
-
-        def gather_words(h):
-            nc.vector.tensor_copy(
-                pair_words[:, h * GATHER : (h + 1) * GATHER].bitcast(U32), token_words[:].bitcast(U32).indirect(entries(h))
-            )
-
-        def part_passes(h):
-            nc.vector.tensor_copy(
-                slot_words[h][:].bitcast(U16),
-                pair_words[:, h * GATHER : (h + 1) * GATHER].bitcast(U16).rearrange("p (c g) -> p g c", g=PASSES),
-            )
 
         def staging(i):
             e, g, n0, n1 = PIECES[i]
@@ -149,10 +134,9 @@ def tile_moe_s_lin_relu_kernel(tc, x_words, x_scales, w, offs, out):
 
         def multiply(sums, tile, g, n0, n1, opens, closes):
             block = tile // TILES_AN_EXPERT * PASSES + g
-            h, first = divmod(tile * P, GATHER)
             nc.tensor.matmul_mx(
                 out=sums,
-                lhsT=slot_words[h][:, g, 2 * first : 2 * (first + P)].bitcast(FP4X4),
+                lhsT=slot_words[:, g, 2 * tile * P : 2 * (tile + 1) * P].bitcast(FP4X4),
                 lhsT_scale=slot_scales[g][:, tile * P : (tile + 1) * P],
                 rhs=codes[:, block, n0:n1].bitcast(FP8X4),
                 rhs_scale=scales[:, block, n0:n1],
@@ -182,32 +166,19 @@ def tile_moe_s_lin_relu_kernel(tc, x_words, x_scales, w, offs, out):
         def relu_on_vector(result, bank):
             nc.vector.tensor_scalar_max(result, bank, 0.0)
 
-        for h in range(SLOTS // GATHER):
-            gather_words(h)
-        for h in range(SLOTS // GATHER):
-            part_passes(h)
-
-        round_piece(0)
-        quantise(0)
-        multiply_expert(0, 0)
-        round_piece(1)
-        round_piece(2)
-        quantise(1)
-        multiply_expert(0, 1)
-        quantise(2)
-        multiply_expert(1, 0)
-        round_piece(3)
+        for i in range(EARLY):
+            round_piece(i)
+        for i in range(EARLY - 1):
+            quantise(i)
+            multiply_expert(*PIECES[i][:2])
+        round_piece(4)
         relu_on_scalar(first_results[:, 0, :], banks[0][:])
         relu_on_scalar(first_results[:, 1, :], banks[1][:])
         quantise(3)
         multiply_expert(1, 1)
 
-        round_piece(4)
-        relu_on_scalar(first_results[:, 3, :], banks[3][:])
         quantise(4)
         multiply_expert(2, 0)
-        relu_on_vector(first_results[:, 2, :], banks[2][:])
-        nc.sync.dma_start(out_tiles[:, 0:4, :], first_results)
         round_and_interleave(nc.scalar.copy, staging(5), raws[5], VECTOR_COLUMNS[5], N)
         round_and_interleave(nc.vector.tensor_copy, staging(5), raws[5], 0, HALF)
         round_and_interleave(nc.vector.tensor_copy, staging(5), raws[5], HALF, VECTOR_COLUMNS[5])
@@ -215,6 +186,9 @@ def tile_moe_s_lin_relu_kernel(tc, x_words, x_scales, w, offs, out):
             quantise_columns(5, n0, n0 + HALF)
             multiply(banks[4][:, n0 : n0 + HALF], 4, 1, n0, n0 + HALF, False, n0 == HALF)
         multiply(banks[5][:], 5, 1, 0, N, False, True)
+        relu_on_scalar(first_results[:, 3, :], banks[3][:])
+        relu_on_vector(first_results[:, 2, :], banks[2][:])
+        nc.sync.dma_start(out_tiles[:, 0:4, :], first_results)
 
         round_piece(6)
         relu_on_scalar(middle_results[:, 0, :], banks[4][:])

@@ -28,15 +28,14 @@ SCALE_ROWS = 4
 QUADRANT = 32
 HALF = N // 2
 AXI = 256
-LEAD = 128
 
 PIECES = (
     [(e, g, 0, N) for e in range(E - 1) for g in range(PASSES)]
     + [(3, g, n0, n0 + HALF) for n0 in (0, HALF) for g in range(PASSES)]
 )
-EARLY = 4
-VECTOR_COLUMNS = [0, 0, 0, 0, 320, 320, 0, 256, 192, 192]
-SCALAR_CUTS = {4: N - LEAD}
+SCALAR_COLUMNS = [512, 512, 512, 416, 192, 192, 256, 0, 64, 64]
+SCALAR_CUTS = {4: 64, 5: 128}
+RESULT_STEP = 704
 
 
 def round_and_interleave(copy, staged, raw, c0, c1):
@@ -79,12 +78,9 @@ def tile_moe_s_lin_relu_kernel(tc, x_words, x_scales, w, offs, out):
         nc.vector.memset(token_scales[:, PASSES * T :].bitcast(I32), 0)
         nc.vector.memset(token_words[:, T:], 0)
 
-        early = keep.tile([P, floats(PIECES[:EARLY])], F32, name="early", align_bytes=AXI)
-        for i in range(EARLY):
-            load(i, early, 0)
-        late = keep.tile([P, LEAD + floats(PIECES[EARLY:])], F32, name="late", align_bytes=AXI)
-        for i in range(EARLY, len(PIECES)):
-            load(i, late[:, LEAD:], EARLY)
+        weights = keep.tile([P, floats(PIECES)], F32, name="weights", align_bytes=AXI)
+        for i in range(len(PIECES)):
+            load(i, weights, 0)
 
         pair_words = keep.tile([P, SLOTS], I32, name="pair_words", align_bytes=64)
         slot_words = keep.tile([P, PASSES, 2 * SLOTS], U8, name="slot_words", align_bytes=64)
@@ -101,7 +97,8 @@ def tile_moe_s_lin_relu_kernel(tc, x_words, x_scales, w, offs, out):
         banks = [psum.tile([P, N], F32, name="bank_%d" % tile) for tile in range(SLOT_TILES)]
         out_tiles = out.rearrange("(s p) n -> p s n", p=P)
 
-        first_results = late[:, 0 : 8 * N].rearrange("p (s n) -> p s n", s=4)[:, :, 0:N]
+        start = floats(PIECES[:4]) + SCALAR_CUTS[4] - N
+        first_results = weights[:, start : start + 4 * RESULT_STEP].rearrange("p (s n) -> p s n", s=4)[:, :, 0:N]
         middle_results = raws[0][:, 0:PACK:2, :]
         low_results = raws[7][:, 0:PACK:2, :]
 
@@ -110,16 +107,13 @@ def tile_moe_s_lin_relu_kernel(tc, x_words, x_scales, w, offs, out):
             block = (e * PASSES + g) * N
             return staged[:, block + n0 : block + n1, :]
 
-        def round_piece(i):
-            width = PIECES[i][3] - PIECES[i][2]
-            share = VECTOR_COLUMNS[i]
-            cut = SCALAR_CUTS.get(i, width)
-            if share < cut:
-                round_and_interleave(nc.scalar.copy, staging(i), raws[i], share, cut)
-            if cut < width:
-                round_and_interleave(nc.scalar.copy, staging(i), raws[i], cut, width)
-            if share:
-                round_and_interleave(nc.vector.tensor_copy, staging(i), raws[i], 0, share)
+        def round_on_scalar(i):
+            cuts = [0, SCALAR_CUTS[i], SCALAR_COLUMNS[i]] if i in SCALAR_CUTS else [0, SCALAR_COLUMNS[i]]
+            for c0, c1 in zip(cuts, cuts[1:]):
+                round_and_interleave(nc.scalar.copy, staging(i), raws[i], c0, c1)
+
+        def round_on_vector(i, c0, c1):
+            round_and_interleave(nc.vector.tensor_copy, staging(i), raws[i], c0, c1)
 
         def quantise_columns(i, c0, c1):
             e, g, n0, n1 = PIECES[i]
@@ -166,54 +160,56 @@ def tile_moe_s_lin_relu_kernel(tc, x_words, x_scales, w, offs, out):
         def relu_on_vector(result, bank):
             nc.vector.tensor_scalar_max(result, bank, 0.0)
 
-        for i in range(EARLY):
-            round_piece(i)
-        for i in range(EARLY - 1):
+        for i in range(4):
+            round_on_scalar(i)
+        for i in range(3):
             quantise(i)
             multiply_expert(*PIECES[i][:2])
-        round_piece(4)
-        relu_on_scalar(first_results[:, 0, :], banks[0][:])
-        relu_on_scalar(first_results[:, 1, :], banks[1][:])
+        round_on_vector(3, SCALAR_COLUMNS[3], N)
         quantise(3)
         multiply_expert(1, 1)
 
+        round_on_scalar(4)
+        round_on_vector(4, SCALAR_COLUMNS[4], N)
+        relu_on_scalar(first_results[:, 0, :], banks[0][:])
+        relu_on_scalar(first_results[:, 1, :], banks[1][:])
+        relu_on_vector(first_results[:, 2, :], banks[2][:])
         quantise(4)
         multiply_expert(2, 0)
-        round_and_interleave(nc.scalar.copy, staging(5), raws[5], VECTOR_COLUMNS[5], N)
-        round_and_interleave(nc.vector.tensor_copy, staging(5), raws[5], 0, HALF)
-        round_and_interleave(nc.vector.tensor_copy, staging(5), raws[5], HALF, VECTOR_COLUMNS[5])
-        for n0 in (0, HALF):
-            quantise_columns(5, n0, n0 + HALF)
-            multiply(banks[4][:, n0 : n0 + HALF], 4, 1, n0, n0 + HALF, False, n0 == HALF)
-        multiply(banks[5][:], 5, 1, 0, N, False, True)
+        round_on_scalar(5)
+        round_on_vector(5, HALF, N)
+        round_on_vector(5, SCALAR_COLUMNS[5], HALF)
         relu_on_scalar(first_results[:, 3, :], banks[3][:])
-        relu_on_vector(first_results[:, 2, :], banks[2][:])
         nc.sync.dma_start(out_tiles[:, 0:4, :], first_results)
+        for n0 in (HALF, 0):
+            quantise_columns(5, n0, n0 + HALF)
+            multiply(banks[4][:, n0 : n0 + HALF], 4, 1, n0, n0 + HALF, False, n0 == 0)
+        multiply(banks[5][:], 5, 1, 0, N, False, True)
 
-        round_piece(6)
+        round_on_scalar(6)
         relu_on_scalar(middle_results[:, 0, :], banks[4][:])
         relu_on_scalar(middle_results[:, 1, :], banks[5][:])
         nc.sync.dma_start(out_tiles[:, 4:6, :], middle_results)
-        round_piece(7)
+        round_on_vector(7, 0, HALF)
         quantise(6)
         multiply_low(0)
         quantise(7)
         multiply_low(1)
-        round_piece(8)
+        round_on_scalar(8)
+        round_on_vector(8, SCALAR_COLUMNS[8], HALF)
         relu_on_scalar(low_results, banks[6][:].rearrange("p (s n) -> p s n", s=2))
         nc.sync.dma_start(out_tiles[:, 6:8, 0:HALF], low_results)
         quantise(8)
         multiply_high(0, 0)
         multiply_high(0, P)
-        round_and_interleave(nc.scalar.copy, staging(9), raws[9], VECTOR_COLUMNS[9], HALF)
-        round_and_interleave(nc.vector.tensor_copy, staging(9), raws[9], 0, P)
-        round_and_interleave(nc.vector.tensor_copy, staging(9), raws[9], P, VECTOR_COLUMNS[9])
-        quantise_columns(9, 0, P)
-        multiply_high(1, 0)
-        quantise_columns(9, P, HALF)
-        multiply_high(1, P)
+        round_on_scalar(9)
+        round_on_vector(9, P, HALF)
+        round_on_vector(9, SCALAR_COLUMNS[9], P)
+        for c0 in (P, 0):
+            quantise_columns(9, c0, c0 + P)
+            multiply_high(1, c0)
 
-        for c0 in (0, P):
+        for c0 in (P, 0):
             relu_on_vector(high_results[:, 0, c0 : c0 + P], high_banks[c0][0][:, 0:P])
             relu_on_scalar(high_results[:, 1, c0 : c0 + P], high_banks[c0][1][:, 0:P])
         nc.sync.dma_start(out_tiles[:, 6:8, HALF:N], high_results[:])

from contextlib import ExitStack

import concourse.mybir as mybir

K, T, E, C, N = 1024, 1024, 4, 256, 512
FLOPS = 2 * E * C * K * N

F32 = mybir.dt.float32
BF16 = mybir.dt.bfloat16
I32 = mybir.dt.int32
U32 = mybir.dt.uint32
U16 = mybir.dt.uint16
U8 = mybir.dt.uint8
FP8X4 = mybir.dt.float8_e4m3fn_x4
FP4X4 = mybir.dt.float4_e2m1fn_x4
RELU = mybir.ActivationFunctionType.Relu

P = 128
PACK = 4
K_PASS = P * PACK
PASSES = K // K_PASS
SLOTS = E * C
SLOT_TILES = SLOTS // P
TILES_AN_EXPERT = C // P
GROUP = 16
SPARE = 512
SCALE_ROWS = 4
QUADRANT = 32
HALF = N // 2
AXI = 256

PIECES = (
    [(e, g, 0, N) for e in range(E - 1) for g in range(PASSES)]
    + [(3, g, n0, n0 + HALF) for n0 in (0, HALF) for g in range(PASSES)]
)
SCALAR_COLUMNS = [512, 512, 512, 416, 192, 192, 256, 0, 64, 64]
SCALAR_CUTS = {4: 64, 5: 128}
RESULT_STEP = 704


def round_and_interleave(copy, staged, raw, c0, c1):
    copy(
        out=staged[:, c0:c1, :].rearrange("p (c i) t -> p c t i", i=2),
        in_=raw[:, :, c0:c1].rearrange("p t (c i) -> p c t i", i=2),
    )


def tile_moe_s_lin_relu_kernel(tc, x_words, x_scales, w, offs, out):
    nc = tc.nc
    with ExitStack() as ctx:
        keep = ctx.enter_context(tc.tile_pool(name="keep", bufs=1))
        psum = ctx.enter_context(tc.psum_pool(name="psum", bufs=1))

        raws = []

        def floats(pieces):
            return PACK * sum(n1 - n0 for e, g, n0, n1 in pieces)

        def load(i, home, first):
            e, g, n0, n1 = PIECES[i]
            at = floats(PIECES[first:i])
            raw = home[:, at : at + PACK * (n1 - n0)].rearrange("p (t n) -> p t n", t=PACK)
            nc.sync.dma_start(raw, w[e, g * K_PASS : (g + 1) * K_PASS, n0:n1].rearrange("(p t) n -> p t n", t=PACK))
            raws.append(raw)

        token_words = keep.tile([P, T + SPARE], I32, name="token_words", align_bytes=AXI)
        nc.sync.dma_start(token_words[:, 0:T], x_words[0].rearrange("p t d -> p (t d)").bitcast(I32))
        offsets = keep.tile([P, SLOTS // GROUP], U16, name="offsets", align_bytes=AXI)
        nc.sync.dma_start(offsets[:], offs)

        token_scales = keep.tile([P, PASSES * T + SPARE], U8, name="token_scales", align_bytes=AXI)
        nc.vector.memset(token_scales[:, 0 : PASSES * T].bitcast(I32), 0)
        for r in range(SCALE_ROWS):
            nc.sync.dma_start(
                token_scales[r:P:QUADRANT, 0 : PASSES * T].bitcast(I32).rearrange("q (g t) -> q g t", g=PASSES),
                x_scales[:, r::SCALE_ROWS, :].rearrange("g q t -> q g t").bitcast(I32),
            )
        nc.vector.memset(token_scales[:, PASSES * T :].bitcast(I32), 0)
        nc.vector.memset(token_words[:, T:], 0)

        weights = keep.tile([P, floats(PIECES)], F32, name="weights", align_bytes=AXI)
        for i in range(len(PIECES)):
            load(i, weights, 0)

        pair_words = keep.tile([P, SLOTS], I32, name="pair_words", align_bytes=64)
        slot_words = keep.tile([P, PASSES, 2 * SLOTS], U8, name="slot_words", align_bytes=64)
        slot_scales = [keep.tile([P, SLOTS], U8, name="slot_scales_%d" % g, align_bytes=64) for g in range(PASSES)]
        nc.vector.tensor_copy(pair_words[:].bitcast(U32), token_words[:].bitcast(U32).indirect(offsets[:]))
        for g in range(PASSES):
            nc.vector.tensor_copy(slot_scales[g][:], token_scales[:, g * T : (g + 1) * T + SPARE].indirect(offsets[:]))
        nc.vector.tensor_copy(slot_words[:].bitcast(U16), pair_words[:].bitcast(U16).rearrange("p (c g) -> p g c", g=PASSES))

        staged = keep.tile([P, E * PASSES * N, PACK], BF16, name="staged", align_bytes=64)
        codes = keep.tile([P, E * PASSES, N], U32, name="codes", align_bytes=64)
        scales = keep.tile([P, E * PASSES, N], U8, name="scales", align_bytes=64)
        high_results = keep.tile([P, TILES_AN_EXPERT, HALF], F32, name="high_results", align_bytes=AXI)
        banks = [psum.tile([P, N], F32, name="bank_%d" % tile) for tile in range(SLOT_TILES)]
        out_tiles = out.rearrange("(s p) n -> p s n", p=P)

        start = floats(PIECES[:4]) + SCALAR_CUTS[4] - N
        first_results = weights[:, start : start + 4 * RESULT_STEP].rearrange("p (s n) -> p s n", s=4)[:, :, 0:N]
        middle_results = raws[0][:, 0:PACK:2, :]
        low_results = raws[7][:, 0:PACK:2, :]

        def staging(i):
            e, g, n0, n1 = PIECES[i]
            block = (e * PASSES + g) * N
            return staged[:, block + n0 : block + n1, :]

        def round_on_scalar(i):
            cuts = [0, SCALAR_CUTS[i], SCALAR_COLUMNS[i]] if i in SCALAR_CUTS else [0, SCALAR_COLUMNS[i]]
            for c0, c1 in zip(cuts, cuts[1:]):
                round_and_interleave(nc.scalar.copy, staging(i), raws[i], c0, c1)

        def round_on_vector(i, c0, c1):
            round_and_interleave(nc.vector.tensor_copy, staging(i), raws[i], c0, c1)

        def quantise_columns(i, c0, c1):
            e, g, n0, n1 = PIECES[i]
            nc.vector.quantize_mx(
                out=codes[:, e * PASSES + g, n0 + c0 : n0 + c1].bitcast(FP8X4),
                scales=scales[:, e * PASSES + g, n0 + c0 : n0 + c1],
                in_=staging(i)[:, c0:c1, :].rearrange("p n t -> p (n t)"),
            )

        def quantise(i):
            quantise_columns(i, 0, PIECES[i][3] - PIECES[i][2])

        def multiply(sums, tile, g, n0, n1, opens, closes):
            block = tile // TILES_AN_EXPERT * PASSES + g
            nc.tensor.matmul_mx(
                out=sums,
                lhsT=slot_words[:, g, 2 * tile * P : 2 * (tile + 1) * P].bitcast(FP4X4),
                lhsT_scale=slot_scales[g][:, tile * P : (tile + 1) * P],
                rhs=codes[:, block, n0:n1].bitcast(FP8X4),
                rhs_scale=scales[:, block, n0:n1],
                start=opens,
                stop=closes,
            )

        def multiply_expert(e, g):
            for tile in range(e * TILES_AN_EXPERT, (e + 1) * TILES_AN_EXPERT):
                multiply(banks[tile][:], tile, g, 0, N, g == 0, g == 1)

        def multiply_low(g):
            for j in range(TILES_AN_EXPERT):
                for c0 in (0, P):
                    at = j * HALF + c0
                    multiply(banks[6][:, at : at + P], 6 + j, g, c0, c0 + P, g == 0 and at == 0, g == 1 and at == N - P)

        high_banks = {0: [banks[7], banks[0]], P: [banks[1], banks[2]]}

        def multiply_high(g, c0):
            for j in range(TILES_AN_EXPERT):
                multiply(high_banks[c0][j][:, 0:P], 6 + j, g, HALF + c0, HALF + c0 + P, g == 0, g == 1)

        def relu_on_scalar(result, bank):
            nc.scalar.activation(result, bank, RELU)

        def relu_on_vector(result, bank):
            nc.vector.tensor_scalar_max(result, bank, 0.0)

        for i in range(4):
            round_on_scalar(i)
        for i in range(3):
            quantise(i)
            multiply_expert(*PIECES[i][:2])
        round_on_vector(3, SCALAR_COLUMNS[3], N)
        quantise(3)
        multiply_expert(1, 1)

        round_on_scalar(4)
        round_on_vector(4, SCALAR_COLUMNS[4], N)
        relu_on_scalar(first_results[:, 0, :], banks[0][:])
        relu_on_scalar(first_results[:, 1, :], banks[1][:])
        relu_on_vector(first_results[:, 2, :], banks[2][:])
        quantise(4)
        multiply_expert(2, 0)
        round_on_scalar(5)
        round_on_vector(5, HALF, N)
        round_on_vector(5, SCALAR_COLUMNS[5], HALF)
        relu_on_scalar(first_results[:, 3, :], banks[3][:])
        nc.sync.dma_start(out_tiles[:, 0:4, :], first_results)
        for n0 in (HALF, 0):
            quantise_columns(5, n0, n0 + HALF)
            multiply(banks[4][:, n0 : n0 + HALF], 4, 1, n0, n0 + HALF, False, n0 == 0)
        multiply(banks[5][:], 5, 1, 0, N, False, True)

        round_on_scalar(6)
        relu_on_scalar(middle_results[:, 0, :], banks[4][:])
        relu_on_scalar(middle_results[:, 1, :], banks[5][:])
        nc.sync.dma_start(out_tiles[:, 4:6, :], middle_results)
        round_on_vector(7, 0, HALF)
        quantise(6)
        multiply_low(0)
        quantise(7)
        multiply_low(1)
        round_on_scalar(8)
        round_on_vector(8, SCALAR_COLUMNS[8], HALF)
        relu_on_scalar(low_results, banks[6][:].rearrange("p (s n) -> p s n", s=2))
        nc.sync.dma_start(out_tiles[:, 6:8, 0:HALF], low_results)
        quantise(8)
        multiply_high(0, 0)
        multiply_high(0, P)
        round_on_scalar(9)
        round_on_vector(9, P, HALF)
        round_on_vector(9, SCALAR_COLUMNS[9], P)
        for c0 in (P, 0):
            quantise_columns(9, c0, c0 + P)
            multiply_high(1, c0)

        for c0 in (P, 0):
            relu_on_vector(high_results[:, 0, c0 : c0 + P], high_banks[c0][0][:, 0:P])
            relu_on_scalar(high_results[:, 1, c0 : c0 + P], high_banks[c0][1][:, 0:P])
        nc.sync.dma_start(out_tiles[:, 6:8, HALF:N], high_results[:])
